import numpy as np
CORES = [33,38,57,62,81,86,161,166,185,190,209,214]
N = 12
T = 2048
def entries(a): return a.T.reshape(-1)
def pack(v, P): return np.ascontiguousarray(np.asarray(v, np.int32).reshape(-1, P).T)
def lists(rng, how):
    h = rng.integers(0, N * T, 8)
    if how == "zero": h[:] = 0
    if how == "blocks": h = T * rng.integers(1, N, 8)
    if how == "last": h[:] = N * T - 1
    if how == "mixed": h = T * rng.choice([q for q in range(N) if q & (q - 1)], 8) + rng.integers(1, T, 8)
    if how == "small": h = rng.permutation([0, 1, T - 1, T, T + 1, N * T - 1, T * int(rng.integers(2, N)), int(rng.integers(1, T))])
    return {"hh": np.broadcast_to(pack(np.concatenate([h, np.zeros(24, np.int64)]), 16), (N, 16, 2)).copy()}
def setup_inputs(rng):
    return dict({"x": rng.standard_normal((N, 128, T), dtype=np.float32)}, **lists(rng, "uniform"))
def setup_inputs_blocks(rng):
    d = setup_inputs(rng); d.update(lists(rng, "blocks"))
    for k in ("x",): d[k] = (d[k].astype(np.float32) * 1048576.0).astype(d[k].dtype)
    return d
def setup_inputs_last(rng):
    d = setup_inputs(rng); d.update(lists(rng, "last"))
    for k in ("x",): d[k] = (d[k].astype(np.float32) * (1 / 1024.0)).astype(d[k].dtype)
    return d
def setup_inputs_mixed(rng):
    d = setup_inputs(rng); d.update(lists(rng, "mixed"))
    return d
def setup_inputs_small(rng):
    d = setup_inputs(rng); d.update(lists(rng, "small"))
    return d
def setup_inputs_zero(rng):
    d = setup_inputs(rng); d.update(lists(rng, "zero"))
    return d
def check_inputs(x):
    bad = []
    if x["hh"].min() < 0 or x["hh"].max() >= N * T: bad.append("hh out of range")
    if entries(x["hh"][0])[8:].any(): bad.append("an entry that should be 0 isn't")
    if not all(np.array_equal(a, x["hh"][0]) for a in x["hh"]): bad.append("hh isn't alike on all ranks")
    return bad
def reference(x, hh):
    h = entries(hh[0]); A = np.concatenate(list(x), axis=1)
    Y = np.concatenate([np.roll(A[16 * k:16 * k + 16], -int(h[k]), axis=1) for k in range(8)], axis=0)
    return {"y": np.stack([Y[:, T * r:T * r + T] for r in range(N)])}

@@ -1,0 +1,336 @@
+from concourse.bass import DstId, RemoteDMATransfer
+from concourse.mybir import AluOpType, ActivationFunctionType
+
+SIM = 256
+COLS = 2048
+NR = 12
+J = 32
+W = COLS // J
+UNIT = 8
+UW = UNIT * W
+OC = NR * W // 16
+
+SCRATCH = {
+    "xs": ("sbuf", [128, COLS], "float32"),
+    "rx": ("sbuf", [128, UW], "float32"),
+    "win": ("sbuf", [128, NR * W], "float32"),
+    "wout": ("sbuf", [128, NR * W], "float32"),
+    "z": ("sbuf", [128, COLS], "float32"),
+    "yo": ("sbuf", [128, COLS], "float32"),
+    "hraw": ("sbuf", [128, 2], "int32"),
+    "oh": ("sbuf", [128, 128], "float32"),
+    "rhs": ("sbuf", [128, 2], "float32"),
+    "si": ("sbuf", [128, 2], "int32"),
+    "pi": ("sbuf", [128, 1], "int32"),
+    "pm": ("sbuf", [128, 1], "int32"),
+    "pf": ("sbuf", [128, 1], "float32"),
+    "sc": ("sbuf", [128, 2], "float32"),
+    "ia": ("sbuf", [128, 128], "int32"),
+    "ib": ("sbuf", [128, OC], "int32"),
+    "fa": ("sbuf", [128, OC], "float32"),
+    "fb": ("sbuf", [128, OC], "float32"),
+    "fu": ("sbuf", [128, OC], "float32"),
+    "fm": ("sbuf", [128, OC], "float32"),
+    "ic": ("sbuf", [128, 128], "int32"),
+    "id2": ("sbuf", [128, 128], "int32"),
+    "off": ("sbuf", [128, 128], "uint16"),
+    "ps": ("psum", [128, 2], "float32"),
+}
+SEMAPHORES = ["hl", "xl0", "xl1", "xl2", "xl3", "ls", "hs", "xr", "da", "za", "vz", "vo", "vs", "gk", "ms",
+              "gv1", "gs1", "gv2", "gs2", "st"]
+
+_PLAN = {}
+
+
+def _bits(mask):
+    return [1 << b for b in range(mask.bit_length()) if (mask >> b) & 1]
+
+
+def _or(bits):
+    m = 0
+    for b in bits:
+        m |= b
+    return m
+
+
+def _plan(T, topo):
+    if _PLAN:
+        return _PLAN
+    ranks = [int(c) for c in T.cores]
+
+    def place(c):
+        return (topo.host(c), topo.chip(c))
+
+    chips = {}
+    for c in range(SIM):
+        chips.setdefault(place(c), []).append(c)
+    rank_chips = set(place(c) for c in ranks)
+
+    def own_plane(a, b):
+        return place(a) == place(b) or topo.same_plane(a, b)
+
+    rot = []
+    for plane in (True, False):
+        cand = []
+        for key in sorted(chips):
+            if key in rank_chips or own_plane(chips[key][0], ranks[0]) != plane:
+                continue
+            mate = any(topo.mates(chips[key][0], r) for r in ranks)
+            cand.append((not mate, key[1], key[0]))
+        cand = sorted(cand)[:UNIT]
+        for half in range(2):
+            for i, (_m, ch, ho) in enumerate(cand):
+                cores = chips[(ho, ch)]
+                for c in cores:
+                    if topo.die(c) == (half + i) % 2 and all(topo.may_write(c, r) for r in ranks):
+                        rot.append(c)
+                        break
+    send = {}
+    helpers = {}
+    for ri, r in enumerate(ranks):
+        team = [c for c in chips[place(r)] if topo.die(c) == topo.die(r)]
+        reach_all = [c for c in team if all(topo.may_write(c, d) for d in rot)]
+        rest = [c for c in team if c not in reach_all]
+        near = [u for u in range(J // UNIT) if own_plane(rot[u * UNIT], r)]
+        far = [u for u in range(J // UNIT) if u not in near]
+        for c, u in list(zip(rest, near)) + list(zip(reach_all, far)):
+            send[c] = (ri, u)
+        helpers[r] = [c for c in team if c != r]
+    taken = {}
+
+    def place_rotator(j, seen):
+        for r in ranks:
+            for c in helpers[r]:
+                if send[c][1] != j // UNIT or c in seen:
+                    continue
+                seen.add(c)
+                if c not in taken or place_rotator(taken[c], seen):
+                    taken[c] = j
+                    return True
+        return False
+
+    for j in range(J):
+        if not place_rotator(j, set()):
+            raise ValueError("no way for hh to rotator %d" % j)
+    for r in ranks:
+        helpers[r] = sorted(helpers[r], key=lambda c: (c in taken, c))
+    _PLAN.update({"ranks": ranks, "rot": rot, "send": send, "helpers": helpers, "hnext": taken})
+    return _PLAN
+
+
+def _xfer(T, topo, src_core, dst_core, mask, sem, src, dst):
+    rid, pid = topo.addr(dst_core, src_core)
+    return RemoteDMATransfer(dst_ids=[DstId(rid=rid, pnc=pid)], dma_engine_mask=mask, remote_sem=sem,
+                             srcs=[src], dsts=[dst])
+
+
+def _send_unit(g, core, T, topo, P, ri, unit, buf, base):
+    tr = []
+    for i in range(UNIT):
+        d = P["rot"][unit * UNIT + i]
+        e = _bits(topo.mask(core, d))
+        tr.append(_xfer(T, topo, core, d, e[i], T.sem.da,
+                        buf[:, base + i * W:base + (i + 1) * W], T.win[:, ri * W:(ri + 1) * W]))
+    g.remote_dma_fused(tr, local_sem=T.sem.ls)
+    return UNIT
+
+
+def _second_turn(j):
+    return j % NR
+
+
+def _phase2(j):
+    return [(list(range(0, 8)), 1), (list(range(8, 12)), 2)]
+
+
+def _onehot(g, T):
+    a = T.oh[0:16, :]
+    g.vector.memset(a, 1.0).then_inc(T.sem.vo, 1)
+    g.wait_ge(T.sem.vo, 1)
+    g.affine_select(a, a, [[1, 128]], AluOpType.is_ge, 0.0, 0, -16).then_inc(T.sem.gk, 1)
+    g.wait_ge(T.sem.gk, 1)
+    g.affine_select(a, a, [[-1, 128]], AluOpType.is_ge, 0.0, 15, 16).then_inc(T.sem.gk, 1)
+
+
+def _lists(g, T, hsem, hval, gk, rotator):
+    v = g.vector
+    n = [0]
+
+    def inc(ins):
+        ins.then_inc(T.sem.vs, 1)
+        n[0] += 1
+
+    def sync():
+        v.wait_ge(T.sem.vs, n[0])
+
+    op = AluOpType
+    v.wait_ge(T.sem.gk, gk)
+    inc(v.tensor_scalar(T.pm[:, 0:1], T.pi[:, 0:1], 15, None, op.bitwise_and))
+    sync()
+    inc(v.tensor_copy(T.pf[:, 0:1], T.pm[:, 0:1]))
+    sync()
+    v.wait_ge(hsem, hval)
+    inc(v.tensor_scalar(T.si[0:16, 0:1], T.hraw[0:16, 0:1], COLS - 1, None, op.bitwise_and))
+    inc(v.tensor_scalar(T.si[0:16, 1:2], T.hraw[0:16, 0:1], 11, None, op.arith_shift_right))
+    sync()
+    inc(v.tensor_copy(T.rhs[0:16, 0:1], T.si[0:16, 0:1]))
+    inc(v.tensor_scalar(T.rhs[0:16, 1:2], T.si[0:16, 1:2], float(W), None, op.mult))
+    sync()
+    g.tensor.wait_ge(T.sem.vs, n[0])
+    g.tensor.matmul(T.ps[:, 0:2], T.oh[0:16, :], T.rhs[0:16, 0:2], True, True).then_inc(T.sem.ms, 1)
+    v.wait_ge(T.sem.ms, 1)
+    if rotator:
+        inc(v.tensor_tensor(T.sc[:, 0:1], T.ps[:, 0:1], T.pf[:, 0:1], op.subtract))
+        inc(v.tensor_tensor(T.sc[:, 1:2], T.ps[:, 1:2], T.pf[:, 0:1], op.add))
+        sync()
+        inc(v.tensor_scalar(T.fa[:, :], T.ia[:, 0:OC], T.sc[:, 0:1], float(W), op.is_lt, op.mult))
+        inc(v.tensor_scalar(T.fb[:, :], T.ib[:, :], T.sc[:, 1:2], None, op.add))
+        sync()
+        inc(v.tensor_tensor(T.fu[:, :], T.fa[:, :], T.fb[:, :], op.add))
+        sync()
+        inc(v.tensor_scalar(T.fm[:, :], T.fu[:, :], float(NR * W), float(-NR * W), op.is_ge, op.mult))
+        sync()
+        inc(v.tensor_tensor(T.fa[:, :], T.fu[:, :], T.fm[:, :], op.add))
+        sync()
+        inc(v.tensor_copy(T.off[:, 0:OC], T.fa[:, :]))
+    else:
+        inc(v.tensor_tensor(T.sc[:, 0:1], T.ps[:, 0:1], T.pf[:, 0:1], op.add))
+        sync()
+        inc(v.tensor_scalar(T.ic[:, :], T.ia[:, :], T.sc[:, 0:1], None, op.add))
+        sync()
+        inc(v.tensor_scalar(T.id2[:, :], T.ic[:, :], COLS - 1, None, op.bitwise_and))
+        sync()
+        inc(v.tensor_copy(T.off[:, :], T.id2[:, :]))
+    return n[0]
+
+
+def _turn(queue, is_vector, out, win, off, sem):
+    if is_vector:
+        queue.tensor_copy(out, win.indirect(off)).then_inc(sem, 1)
+    else:
+        queue.activation(out, win.indirect(off), ActivationFunctionType.Copy).then_inc(sem, 1)
+
+
+def _rank(g, core, T, topo, P):
+    ri = P["ranks"].index(core)
+    own = P["send"][core][1]
+    hp = P["helpers"][core]
+    g.vector.memset(T.hraw[:, :], 0).then_inc(T.sem.vz, 1)
+    units = [P["send"][c][1] for c in hp] + [own]
+    g.sync.wait_ge(T.sem.vz, 1)
+    g.sync.dma_start(T.hraw[0:16, :], T.hh[:, :]).then_inc(T.sem.hl, 16)
+    for i, u in enumerate(units):
+        q = g.scalar if i % 2 == 0 else g.sync
+        q.dma_start(T.xs[:, u * UW:(u + 1) * UW], T.x[:, u * UW:(u + 1) * UW]).then_inc(T.sem["xl%d" % i], 16)
+    ls = 0
+    tr = []
+    g.wait_ge(T.sem.vz, 1)
+    g.wait_ge(T.sem.hl, 16)
+    for i, c in enumerate([c for c in hp if c in P["hnext"]]):
+        e = _bits(topo.mask(core, c))[4 * i:4 * i + 4]
+        tr.append(_xfer(T, topo, core, c, _or(e), T.sem.hs, T.hraw[:, :], T.hraw[:, :]))
+        ls += 4
+    if tr:
+        g.remote_dma_fused(tr, local_sem=T.sem.ls)
+    tr = []
+    for i in range(2):
+        g.wait_ge(T.sem["xl%d" % i], 16)
+        e = _bits(topo.mask(core, hp[i]))[8 * i:8 * i + 8]
+        tr.append(_xfer(T, topo, core, hp[i], _or(e), T.sem.xr, T.xs[:, units[i] * UW:(units[i] + 1) * UW], T.rx[:, :]))
+        ls += 8
+    g.remote_dma_fused(tr, local_sem=T.sem.ls)
+    g.wait_ge(T.sem.xl2, 16)
+    off_chip = _bits(topo.mask(core, P["rot"][own * UNIT]))
+    e = [b for b in _bits(topo.mask(core, hp[2])) if b not in off_chip]
+    g.remote_dma_fused([_xfer(T, topo, core, hp[2], _or(e), T.sem.xr,
+                              T.xs[:, units[2] * UW:(units[2] + 1) * UW], T.rx[:, :])], local_sem=T.sem.ls)
+    ls += len(e)
+    g.wait_ge(T.sem.xl3, 16)
+    ls += _send_unit(g, core, T, topo, P, ri, own, T.xs, own * UW)
+    _onehot(g, T)
+    g.iota(T.pi[:, 0:1], [[0, 1]], 0, 1).then_inc(T.sem.gk, 1)
+    g.iota(T.ia[:, :], [[16, 128]], 0, 0).then_inc(T.sem.gk, 1)
+    nv = _lists(g, T, T.sem.hl, 16, 4, False)
+    za = 0
+    for j in range(J):
+        for slots, ne in _phase2(j):
+            for o in slots:
+                if (_second_turn(j) + o) % NR == ri:
+                    za += ne
+    half, first = COLS // 2, 384
+    for k, (queue, isv) in enumerate(((g.vector, True), (g.scalar, False))):
+        queue.wait_ge(T.sem.vs, nv)
+        queue.wait_ge(T.sem.za, za)
+        a = k * half
+        names = ("gv1", "gv2") if isv else ("gs1", "gs2")
+        for (lo, hi), nm in zip(((a, a + first), (a + first, a + half)), names):
+            _turn(queue, isv, T.yo[:, lo:hi], T.z[:, :], T.off[:, lo // 16:hi // 16], T.sem[nm])
+    for nm, lo, hi in (("gv1", 0, first), ("gs1", half, half + first), ("gv2", first, half)):
+        g.sync.wait_ge(T.sem[nm], 1)
+        g.sync.dma_start(T.y[:, lo:hi], T.yo[:, lo:hi]).then_inc(T.sem.st, 16)
+    g.scalar.wait_ge(T.sem.gs2, 1)
+    g.scalar.dma_start(T.y[:, half + first:], T.yo[:, half + first:]).then_inc(T.sem.st, 16)
+    g.sync.wait_ge(T.sem.st, 64)
+    g.wait_ge(T.sem.ls, ls)
+
+
+def _helper(g, core, T, topo, P):
+    ri, unit = P["send"][core]
+    ls = 0
+    if core in P["hnext"]:
+        d = P["rot"][P["hnext"][core]]
+        rid, pid = topo.addr(d, core)
+        m = topo.mask(core, d)
+        g.wait_ge(T.sem.hs, 4)
+        g.remote_dma(T.hraw[:, :], T.hraw[:, :], T.sem.hs, T.sem.ls, pid, rid, m)
+        ls += len(_bits(m))
+    g.wait_ge(T.sem.xr, 8)
+    ls += _send_unit(g, core, T, topo, P, ri, unit, T.rx, 0)
+    g.wait_ge(T.sem.ls, ls)
+
+
+def _rotator(g, core, T, topo, P):
+    j = P["rot"].index(core)
+    t0 = _second_turn(j)
+    src = [c for c in P["hnext"] if P["hnext"][c] == j][0]
+    nh = len(_bits(topo.mask(src, core)))
+    _onehot(g, T)
+    gk = 2
+    g.iota(T.pi[:, 0:1], [[0, 1]], 0, 1).then_inc(T.sem.gk, 1)
+    g.iota(T.ia[:, 0:OC], [[0, NR], [16, W // 16]], j * W, 0).then_inc(T.sem.gk, 1)
+    gk += 2
+    cut = (NR - t0) * (W // 16)
+    g.iota(T.ib[:, 0:cut], [[W, NR - t0], [16, W // 16]], t0 * W, 0).then_inc(T.sem.gk, 1)
+    gk += 1
+    if t0:
+        g.iota(T.ib[:, cut:OC], [[W, t0], [16, W // 16]], 0, 0).then_inc(T.sem.gk, 1)
+        gk += 1
+    nv = _lists(g, T, T.sem.hs, nh, gk, True)
+    for queue, isv in ((g.vector, True), (g.scalar, False)):
+        queue.wait_ge(T.sem.vs, nv)
+        queue.wait_ge(T.sem.da, NR)
+        parts = ((0, 4, "gv1"), (8, 10, "gv2")) if isv else ((4, 8, "gs1"), (10, 12, "gs2"))
+        for a, b, nm in parts:
+            _turn(queue, isv, T.wout[:, a * W:b * W], T.win[:, :], T.off[:, a * W // 16:b * W // 16], T.sem[nm])
+    ls = 0
+    for k, (slots, ne) in enumerate(_phase2(j)):
+        g.wait_ge(T.sem["gv%d" % (k + 1)], 1)
+        g.wait_ge(T.sem["gs%d" % (k + 1)], 1)
+        tr = []
+        for i, o in enumerate(slots):
+            d = P["ranks"][(t0 + o) % NR]
+            e = _bits(topo.mask(core, d))[i * ne:(i + 1) * ne]
+            tr.append(_xfer(T, topo, core, d, _or(e), T.sem.za, T.wout[:, o * W:(o + 1) * W], T.z[:, j * W:(j + 1) * W]))
+            ls += ne
+        g.remote_dma_fused(tr, local_sem=T.sem.ls)
+    g.wait_ge(T.sem.ls, ls)
+
+
+def rank_program(g, core, T, topo):
+    P = _plan(T, topo)
+    if core in P["ranks"]:
+        _rank(g, core, T, topo, P)
+    elif core in P["send"]:
+        _helper(g, core, T, topo, P)
+    elif core in P["rot"]:
+        _rotator(g, core, T, topo, P)

@@ -7,8 +7,13 @@ NR = 12
 J = 32
 W = COLS // J
 UNIT = 8
+PART = 6
 UW = UNIT * W
 OC = NR * W // 16
+SCALE = COLS // W
+PIECES = ((0, 48), (48, 88), (88, 128))
+PW = 48
+PARTS = (256, 416, 352)
 
 SCRATCH = {
     "xs": ("sbuf", [128, COLS], "float32"),
@@ -19,25 +24,29 @@ SCRATCH = {
     "yo": ("sbuf", [128, COLS], "float32"),
     "hraw": ("sbuf", [128, 2], "int32"),
     "oh": ("sbuf", [128, 128], "float32"),
-    "rhs": ("sbuf", [128, 2], "float32"),
-    "si": ("sbuf", [128, 2], "int32"),
+    "rhs": ("sbuf", [128, 1], "float32"),
     "pi": ("sbuf", [128, 1], "int32"),
     "pm": ("sbuf", [128, 1], "int32"),
     "pf": ("sbuf", [128, 1], "float32"),
-    "sc": ("sbuf", [128, 2], "float32"),
-    "ia": ("sbuf", [128, 128], "int32"),
+    "ia": ("sbuf", [128, OC], "int32"),
     "ib": ("sbuf", [128, OC], "int32"),
-    "fa": ("sbuf", [128, OC], "float32"),
-    "fb": ("sbuf", [128, OC], "float32"),
-    "fu": ("sbuf", [128, OC], "float32"),
-    "fm": ("sbuf", [128, OC], "float32"),
-    "ic": ("sbuf", [128, 128], "int32"),
-    "id2": ("sbuf", [128, 128], "int32"),
-    "off": ("sbuf", [128, 128], "uint16"),
-    "ps": ("psum", [128, 2], "float32"),
+    "ip": ("sbuf", [128, PW], "int32"),
+    "ja": ("sbuf", [128, OC], "float32"),
+    "jb": ("sbuf", [128, OC], "int32"),
+    "jp": ("sbuf", [128, PW], "float32"),
+    "ua": ("sbuf", [128, OC], "int32"),
+    "ub": ("sbuf", [128, OC], "int32"),
+    "uc": ("sbuf", [128, OC], "int32"),
+    "um": ("sbuf", [128, OC], "int32"),
+    "uf": ("sbuf", [128, OC], "float32"),
+    "ic": ("sbuf", [128, PW], "int32"),
+    "id2": ("sbuf", [128, PW], "int32"),
+    "offp": ("sbuf", [128, PW], "uint16"),
+    "off": ("sbuf", [128, COLS // 16], "uint16"),
+    "ps": ("psum", [128, 1], "float32"),
 }
-SEMAPHORES = ["hl", "xl0", "xl1", "xl2", "xl3", "ls", "hs", "xr", "da", "za", "vz", "vo", "vs", "gk", "ms",
-              "gv1", "gs1", "gv2", "gs2", "st"]
+SEMAPHORES = ["hl", "xl0", "xl1", "xl2", "xl3", "ls", "hs", "xr", "da", "za", "lz", "vz", "vo", "vs", "vp", "gk", "ms",
+              "gv0", "gs0", "gv1", "gs1", "gv2", "gs2", "st"]
 
 _PLAN = {}
 
@@ -85,7 +94,7 @@ def _plan(T, topo):
                     if topo.die(c) == (half + i) % 2 and all(topo.may_write(c, r) for r in ranks):
                         rot.append(c)
                         break
-    send = {}
+    unit_of = {}
     helpers = {}
     for ri, r in enumerate(ranks):
         team = [c for c in chips[place(r)] if topo.die(c) == topo.die(r)]
@@ -94,14 +103,24 @@ def _plan(T, topo):
         near = [u for u in range(J // UNIT) if own_plane(rot[u * UNIT], r)]
         far = [u for u in range(J // UNIT) if u not in near]
         for c, u in list(zip(rest, near)) + list(zip(reach_all, far)):
-            send[c] = (ri, u)
-        helpers[r] = [c for c in team if c != r]
+            unit_of[c] = (ri, u)
+        helpers[r] = sorted([c for c in team if c != r], key=lambda c: ((c in rest) == (r in rest), c))
+    calls = {}
+    for r in ranks:
+        hp = helpers[r]
+        for c in hp[:2]:
+            u = unit_of[c][1] * UNIT
+            calls[c] = [([u + i for i in range(UNIT)], 1)]
+        u = unit_of[hp[2]][1] * UNIT
+        calls[hp[2]] = [([u + i for i in range(4)], 2), ([u + i for i in range(4, PART)], 4)]
+        v = unit_of[r][1] * UNIT
+        calls[r] = [([u + i for i in range(PART, UNIT)], 4), ([v + i for i in range(UNIT)], 1)]
     taken = {}
 
     def place_rotator(j, seen):
         for r in ranks:
             for c in helpers[r]:
-                if send[c][1] != j // UNIT or c in seen:
+                if unit_of[c][1] != j // UNIT or c in seen:
                     continue
                 seen.add(c)
                 if c not in taken or place_rotator(taken[c], seen):
@@ -112,9 +131,19 @@ def _plan(T, topo):
     for j in range(J):
         if not place_rotator(j, set()):
             raise ValueError("no way for hh to rotator %d" % j)
+    hnext = {}
+    makers = list(rot)
+    for c in taken:
+        hnext[c] = rot[taken[c]]
+    spare = [c for d in rot for c in chips[place(d)] if c not in rot and all(topo.may_write(c, r) for r in ranks)]
     for r in ranks:
-        helpers[r] = sorted(helpers[r], key=lambda c: (c in taken, c))
-    _PLAN.update({"ranks": ranks, "rot": rot, "send": send, "helpers": helpers, "hnext": taken})
+        for c in helpers[r]:
+            if c not in hnext:
+                d = [d for d in spare if d not in makers and topo.may_write(c, d)][0]
+                hnext[c] = d
+                makers.append(d)
+    _PLAN.update({"ranks": ranks, "rot": rot, "unit_of": unit_of, "calls": calls, "helpers": helpers,
+                  "hnext": hnext, "makers": makers})
     return _PLAN
 
 
@@ -124,15 +153,15 @@ def _xfer(T, topo, src_core, dst_core, mask, sem, src, dst):
                              srcs=[src], dsts=[dst])
 
 
-def _send_unit(g, core, T, topo, P, ri, unit, buf, base):
+def _send_slices(g, core, T, topo, P, ri, slices, ne, buf, first):
     tr = []
-    for i in range(UNIT):
-        d = P["rot"][unit * UNIT + i]
-        e = _bits(topo.mask(core, d))
-        tr.append(_xfer(T, topo, core, d, e[i], T.sem.da,
-                        buf[:, base + i * W:base + (i + 1) * W], T.win[:, ri * W:(ri + 1) * W]))
+    for i, j in enumerate(slices):
+        d = P["rot"][j]
+        e = _bits(topo.mask(core, d))[i * ne:(i + 1) * ne]
+        a = (j - first) * W
+        tr.append(_xfer(T, topo, core, d, _or(e), T.sem.da, buf[:, a:a + W], T.win[:, ri * W:(ri + 1) * W]))
     g.remote_dma_fused(tr, local_sem=T.sem.ls)
-    return UNIT
+    return ne * len(slices)
 
 
 def _second_turn(j):
@@ -141,6 +170,14 @@ def _second_turn(j):
 
 def _phase2(j):
     return [(list(range(0, 8)), 1), (list(range(8, 12)), 2)]
+
+
+def _hh_engines(e, i):
+    return e[4 * i:4 * i + 4]
+
+
+def _unit_engines(e, i, off_chip):
+    return (e[0:8], e[8:16], [b for b in e if b not in off_chip])[i]
 
 
 def _onehot(g, T):
@@ -152,8 +189,16 @@ def _onehot(g, T):
     g.affine_select(a, a, [[-1, 128]], AluOpType.is_ge, 0.0, 15, 16).then_inc(T.sem.gk, 1)
 
 
-def _lists(g, T, hsem, hval, gk, rotator):
+def _make_lists(g, core, T, topo, P, j):
+    op = AluOpType
     v = g.vector
+    m = P["makers"].index(core)
+    d = P["ranks"][m // len(PIECES)]
+    lo, hi = PIECES[m % len(PIECES)]
+    pw = hi - lo
+    src = [c for c in P["hnext"] if P["hnext"][c] == core][0]
+    nh = len(_bits(topo.mask(src, core)))
+    rotator = j is not None
     n = [0]
 
     def inc(ins):
@@ -163,45 +208,58 @@ def _lists(g, T, hsem, hval, gk, rotator):
     def sync():
         v.wait_ge(T.sem.vs, n[0])
 
-    op = AluOpType
+    _onehot(g, T)
+    g.iota(T.pi[:, 0:1], [[0, 1]], 0, 1).then_inc(T.sem.gk, 1)
+    g.iota(T.ip[:, 0:pw], [[16, pw]], 16 * lo, 0).then_inc(T.sem.gk, 1)
+    gk = 4
+    if rotator:
+        t0 = _second_turn(j)
+        g.iota(T.ia[:, :], [[0, NR], [-16, W // 16]], COLS - 1 - j * W, 0).then_inc(T.sem.gk, 1)
+        cut = (NR - t0) * (W // 16)
+        g.iota(T.ib[:, 0:cut], [[W, NR - t0], [16, W // 16]], t0 * W, 0).then_inc(T.sem.gk, 1)
+        gk += 2
+        if t0:
+            g.iota(T.ib[:, cut:OC], [[W, t0], [16, W // 16]], 0, 0).then_inc(T.sem.gk, 1)
+            gk += 1
     v.wait_ge(T.sem.gk, gk)
     inc(v.tensor_scalar(T.pm[:, 0:1], T.pi[:, 0:1], 15, None, op.bitwise_and))
     sync()
     inc(v.tensor_copy(T.pf[:, 0:1], T.pm[:, 0:1]))
     sync()
-    v.wait_ge(hsem, hval)
-    inc(v.tensor_scalar(T.si[0:16, 0:1], T.hraw[0:16, 0:1], COLS - 1, None, op.bitwise_and))
-    inc(v.tensor_scalar(T.si[0:16, 1:2], T.hraw[0:16, 0:1], 11, None, op.arith_shift_right))
-    sync()
-    inc(v.tensor_copy(T.rhs[0:16, 0:1], T.si[0:16, 0:1]))
-    inc(v.tensor_scalar(T.rhs[0:16, 1:2], T.si[0:16, 1:2], float(W), None, op.mult))
-    sync()
-    g.tensor.wait_ge(T.sem.vs, n[0])
-    g.tensor.matmul(T.ps[:, 0:2], T.oh[0:16, :], T.rhs[0:16, 0:2], True, True).then_inc(T.sem.ms, 1)
-    v.wait_ge(T.sem.ms, 1)
     if rotator:
-        inc(v.tensor_tensor(T.sc[:, 0:1], T.ps[:, 0:1], T.pf[:, 0:1], op.subtract))
-        inc(v.tensor_tensor(T.sc[:, 1:2], T.ps[:, 1:2], T.pf[:, 0:1], op.add))
+        inc(v.tensor_scalar(T.ja[:, :], T.ia[:, :], T.pf[:, 0:1], None, op.subtract))
+        inc(v.tensor_scalar(T.jb[:, :], T.ib[:, :], T.pf[:, 0:1], float(SCALE), op.add, op.mult))
+    inc(v.tensor_scalar(T.jp[:, 0:pw], T.ip[:, 0:pw], T.pf[:, 0:1], None, op.add))
+    sync()
+    v.wait_ge(T.sem.hs, nh)
+    inc(v.tensor_copy(T.rhs[0:16, 0:1], T.hraw[0:16, 0:1]))
+    g.tensor.wait_ge(T.sem.vs, n[0])
+    g.tensor.matmul(T.ps[:, 0:1], T.oh[0:16, :], T.rhs[0:16, 0:1], True, True).then_inc(T.sem.ms, 1)
+    v.wait_ge(T.sem.ms, 1)
+    v.tensor_scalar(T.ic[:, 0:pw], T.jp[:, 0:pw], T.ps[:, 0:1], None, op.add).then_inc(T.sem.vp, 1)
+    if rotator:
+        inc(v.tensor_scalar(T.ua[:, :], T.ja[:, :], T.ps[:, 0:1], None, op.add))
+    v.wait_ge(T.sem.vp, 1)
+    v.tensor_scalar(T.id2[:, 0:pw], T.ic[:, 0:pw], COLS - 1, None, op.bitwise_and).then_inc(T.sem.vp, 1)
+    if rotator:
         sync()
-        inc(v.tensor_scalar(T.fa[:, :], T.ia[:, 0:OC], T.sc[:, 0:1], float(W), op.is_lt, op.mult))
-        inc(v.tensor_scalar(T.fb[:, :], T.ib[:, :], T.sc[:, 1:2], None, op.add))
+        inc(v.tensor_scalar(T.ub[:, :], T.ua[:, :], 15 * COLS, None, op.bitwise_and))
+    v.wait_ge(T.sem.vp, 2)
+    v.tensor_copy(T.offp[:, 0:pw], T.id2[:, 0:pw]).then_inc(T.sem.vp, 1)
+    if rotator:
         sync()
-        inc(v.tensor_tensor(T.fu[:, :], T.fa[:, :], T.fb[:, :], op.add))
+        inc(v.tensor_tensor(T.uc[:, :], T.ub[:, :], T.jb[:, :], op.add))
         sync()
-        inc(v.tensor_scalar(T.fm[:, :], T.fu[:, :], float(NR * W), float(-NR * W), op.is_ge, op.mult))
+        inc(v.tensor_scalar(T.um[:, :], T.uc[:, :], float(NR * COLS), float(-NR * COLS), op.is_ge, op.mult))
         sync()
-        inc(v.tensor_tensor(T.fa[:, :], T.fu[:, :], T.fm[:, :], op.add))
+        inc(v.tensor_tensor(T.uf[:, :], T.uc[:, :], T.um[:, :], op.add))
         sync()
-        inc(v.tensor_copy(T.off[:, 0:OC], T.fa[:, :]))
-    else:
-        inc(v.tensor_tensor(T.sc[:, 0:1], T.ps[:, 0:1], T.pf[:, 0:1], op.add))
-        sync()
-        inc(v.tensor_scalar(T.ic[:, :], T.ia[:, :], T.sc[:, 0:1], None, op.add))
-        sync()
-        inc(v.tensor_scalar(T.id2[:, :], T.ic[:, :], COLS - 1, None, op.bitwise_and))
-        sync()
-        inc(v.tensor_copy(T.off[:, :], T.id2[:, :]))
-    return n[0]
+        inc(v.tensor_scalar(T.off[:, 0:OC], T.uf[:, :], 1.0 / SCALE, None, op.mult))
+    g.wait_ge(T.sem.vp, 3)
+    rid, pid = topo.addr(d, core)
+    e = topo.mask(core, d)
+    g.remote_dma(T.off[:, lo:hi], T.offp[:, 0:pw], T.sem.lz, T.sem.ls, pid, rid, e)
+    return n[0], len(_bits(e))
 
 
 def _turn(queue, is_vector, out, win, off, sem):
@@ -211,108 +269,109 @@ def _turn(queue, is_vector, out, win, off, sem):
         queue.activation(out, win.indirect(off), ActivationFunctionType.Copy).then_inc(sem, 1)
 
 
+def _off_chip(topo, P, r):
+    return _bits(topo.mask(r, P["rot"][P["unit_of"][r][1] * UNIT]))
+
+
 def _rank(g, core, T, topo, P):
     ri = P["ranks"].index(core)
-    own = P["send"][core][1]
     hp = P["helpers"][core]
-    g.vector.memset(T.hraw[:, :], 0).then_inc(T.sem.vz, 1)
-    units = [P["send"][c][1] for c in hp] + [own]
-    g.sync.wait_ge(T.sem.vz, 1)
+    g.vector.memset(T.hraw[32:64, :], 0).then_inc(T.sem.vz, 1)
+    g.vector.memset(T.hraw[64:128, :], 0).then_inc(T.sem.vz, 1)
+    units = [P["unit_of"][c][1] for c in hp + [core]]
     g.sync.dma_start(T.hraw[0:16, :], T.hh[:, :]).then_inc(T.sem.hl, 16)
+    g.scalar.dma_start(T.hraw[16:32, :], T.hh[:, :]).then_inc(T.sem.hl, 16)
     for i, u in enumerate(units):
         q = g.scalar if i % 2 == 0 else g.sync
         q.dma_start(T.xs[:, u * UW:(u + 1) * UW], T.x[:, u * UW:(u + 1) * UW]).then_inc(T.sem["xl%d" % i], 16)
     ls = 0
     tr = []
-    g.wait_ge(T.sem.vz, 1)
-    g.wait_ge(T.sem.hl, 16)
-    for i, c in enumerate([c for c in hp if c in P["hnext"]]):
-        e = _bits(topo.mask(core, c))[4 * i:4 * i + 4]
+    g.wait_ge(T.sem.vz, 2)
+    g.wait_ge(T.sem.hl, 32)
+    for i, c in enumerate(hp):
+        e = _hh_engines(_bits(topo.mask(core, c)), i)
         tr.append(_xfer(T, topo, core, c, _or(e), T.sem.hs, T.hraw[:, :], T.hraw[:, :]))
-        ls += 4
-    if tr:
-        g.remote_dma_fused(tr, local_sem=T.sem.ls)
-    tr = []
-    for i in range(2):
-        g.wait_ge(T.sem["xl%d" % i], 16)
-        e = _bits(topo.mask(core, hp[i]))[8 * i:8 * i + 8]
-        tr.append(_xfer(T, topo, core, hp[i], _or(e), T.sem.xr, T.xs[:, units[i] * UW:(units[i] + 1) * UW], T.rx[:, :]))
-        ls += 8
+        ls += len(e)
     g.remote_dma_fused(tr, local_sem=T.sem.ls)
-    g.wait_ge(T.sem.xl2, 16)
-    off_chip = _bits(topo.mask(core, P["rot"][own * UNIT]))
-    e = [b for b in _bits(topo.mask(core, hp[2])) if b not in off_chip]
-    g.remote_dma_fused([_xfer(T, topo, core, hp[2], _or(e), T.sem.xr,
-                              T.xs[:, units[2] * UW:(units[2] + 1) * UW], T.rx[:, :])], local_sem=T.sem.ls)
-    ls += len(e)
-    g.wait_ge(T.sem.xl3, 16)
-    ls += _send_unit(g, core, T, topo, P, ri, own, T.xs, own * UW)
-    _onehot(g, T)
-    g.iota(T.pi[:, 0:1], [[0, 1]], 0, 1).then_inc(T.sem.gk, 1)
-    g.iota(T.ia[:, :], [[16, 128]], 0, 0).then_inc(T.sem.gk, 1)
-    nv = _lists(g, T, T.sem.hl, 16, 4, False)
+    for group in ((0, 1), (2,)):
+        tr = []
+        for i in group:
+            g.wait_ge(T.sem["xl%d" % i], 16)
+            w = UW if i < 2 else PART * W
+            e = _unit_engines(_bits(topo.mask(core, hp[i])), i, _off_chip(topo, P, core))
+            tr.append(_xfer(T, topo, core, hp[i], _or(e), T.sem.xr,
+                            T.xs[:, units[i] * UW:units[i] * UW + w], T.rx[:, 0:w]))
+            ls += len(e)
+        g.remote_dma_fused(tr, local_sem=T.sem.ls)
+    for k, (slices, ne) in enumerate(P["calls"][core]):
+        if k:
+            g.wait_ge(T.sem.xl3, 16)
+        ls += _send_slices(g, core, T, topo, P, ri, slices, ne, T.xs, 0)
     za = 0
     for j in range(J):
         for slots, ne in _phase2(j):
             for o in slots:
                 if (_second_turn(j) + o) % NR == ri:
                     za += ne
-    half, first = COLS // 2, 384
+    lz = 0
+    for m, c in enumerate(P["makers"]):
+        if m // len(PIECES) == ri:
+            lz += len(_bits(topo.mask(c, core)))
     for k, (queue, isv) in enumerate(((g.vector, True), (g.scalar, False))):
-        queue.wait_ge(T.sem.vs, nv)
+        queue.wait_ge(T.sem.lz, lz)
         queue.wait_ge(T.sem.za, za)
-        a = k * half
-        names = ("gv1", "gv2") if isv else ("gs1", "gs2")
-        for (lo, hi), nm in zip(((a, a + first), (a + first, a + half)), names):
-            _turn(queue, isv, T.yo[:, lo:hi], T.z[:, :], T.off[:, lo // 16:hi // 16], T.sem[nm])
-    for nm, lo, hi in (("gv1", 0, first), ("gs1", half, half + first), ("gv2", first, half)):
-        g.sync.wait_ge(T.sem[nm], 1)
-        g.sync.dma_start(T.y[:, lo:hi], T.yo[:, lo:hi]).then_inc(T.sem.st, 16)
-    g.scalar.wait_ge(T.sem.gs2, 1)
-    g.scalar.dma_start(T.y[:, half + first:], T.yo[:, half + first:]).then_inc(T.sem.st, 16)
-    g.sync.wait_ge(T.sem.st, 64)
+        a = 0
+        for i, w in enumerate(PARTS):
+            lo = a + k * w
+            _turn(queue, isv, T.yo[:, lo:lo + w], T.z[:, :], T.off[:, lo // 16:(lo + w) // 16],
+                  T.sem[("gv%d" if isv else "gs%d") % i])
+            a += 2 * w
+    a = 0
+    for i, w in enumerate(PARTS):
+        g.sync.wait_ge(T.sem["gv%d" % i], 1)
+        g.sync.wait_ge(T.sem["gs%d" % i], 1)
+        g.sync.dma_start(T.y[:, a:a + 2 * w], T.yo[:, a:a + 2 * w]).then_inc(T.sem.st, 16)
+        a += 2 * w
+    g.sync.wait_ge(T.sem.st, 16 * len(PARTS))
     g.wait_ge(T.sem.ls, ls)
 
 
 def _helper(g, core, T, topo, P):
-    ri, unit = P["send"][core]
-    ls = 0
-    if core in P["hnext"]:
-        d = P["rot"][P["hnext"][core]]
-        rid, pid = topo.addr(d, core)
-        m = topo.mask(core, d)
-        g.wait_ge(T.sem.hs, 4)
-        g.remote_dma(T.hraw[:, :], T.hraw[:, :], T.sem.hs, T.sem.ls, pid, rid, m)
-        ls += len(_bits(m))
-    g.wait_ge(T.sem.xr, 8)
-    ls += _send_unit(g, core, T, topo, P, ri, unit, T.rx, 0)
+    ri, unit = P["unit_of"][core]
+    r = P["ranks"][ri]
+    i = P["helpers"][r].index(core)
+    d = P["hnext"][core]
+    rid, pid = topo.addr(d, core)
+    m = topo.mask(core, d)
+    g.wait_ge(T.sem.hs, len(_hh_engines(_bits(topo.mask(r, core)), i)))
+    g.remote_dma(T.hraw[:, :], T.hraw[:, :], T.sem.hs, T.sem.ls, pid, rid, m)
+    ls = len(_bits(m))
+    g.wait_ge(T.sem.xr, len(_unit_engines(_bits(topo.mask(r, core)), i, _off_chip(topo, P, r))))
+    for slices, ne in P["calls"][core]:
+        ls += _send_slices(g, core, T, topo, P, ri, slices, ne, T.rx, unit * UNIT)
+    g.wait_ge(T.sem.ls, ls)
+
+
+def _maker(g, core, T, topo, P):
+    _nv, ls = _make_lists(g, core, T, topo, P, None)
     g.wait_ge(T.sem.ls, ls)
 
 
 def _rotator(g, core, T, topo, P):
     j = P["rot"].index(core)
     t0 = _second_turn(j)
-    src = [c for c in P["hnext"] if P["hnext"][c] == j][0]
-    nh = len(_bits(topo.mask(src, core)))
-    _onehot(g, T)
-    gk = 2
-    g.iota(T.pi[:, 0:1], [[0, 1]], 0, 1).then_inc(T.sem.gk, 1)
-    g.iota(T.ia[:, 0:OC], [[0, NR], [16, W // 16]], j * W, 0).then_inc(T.sem.gk, 1)
-    gk += 2
-    cut = (NR - t0) * (W // 16)
-    g.iota(T.ib[:, 0:cut], [[W, NR - t0], [16, W // 16]], t0 * W, 0).then_inc(T.sem.gk, 1)
-    gk += 1
-    if t0:
-        g.iota(T.ib[:, cut:OC], [[W, t0], [16, W // 16]], 0, 0).then_inc(T.sem.gk, 1)
-        gk += 1
-    nv = _lists(g, T, T.sem.hs, nh, gk, True)
+    nv, ls = _make_lists(g, core, T, topo, P, j)
+    da = 0
+    for c in P["calls"]:
+        for slices, ne in P["calls"][c]:
+            if j in slices:
+                da += ne
     for queue, isv in ((g.vector, True), (g.scalar, False)):
         queue.wait_ge(T.sem.vs, nv)
-        queue.wait_ge(T.sem.da, NR)
+        queue.wait_ge(T.sem.da, da)
         parts = ((0, 4, "gv1"), (8, 10, "gv2")) if isv else ((4, 8, "gs1"), (10, 12, "gs2"))
         for a, b, nm in parts:
             _turn(queue, isv, T.wout[:, a * W:b * W], T.win[:, :], T.off[:, a * W // 16:b * W // 16], T.sem[nm])
-    ls = 0
     for k, (slots, ne) in enumerate(_phase2(j)):
         g.wait_ge(T.sem["gv%d" % (k + 1)], 1)
         g.wait_ge(T.sem["gs%d" % (k + 1)], 1)
@@ -330,7 +389,9 @@ def rank_program(g, core, T, topo):
     P = _plan(T, topo)
     if core in P["ranks"]:
         _rank(g, core, T, topo, P)
-    elif core in P["send"]:
+    elif core in P["unit_of"]:
         _helper(g, core, T, topo, P)
     elif core in P["rot"]:
         _rotator(g, core, T, topo, P)
+    elif core in P["makers"]:
+        _maker(g, core, T, topo, P)

@@ -8,45 +8,50 @@ J = 32
 W = COLS // J
 UNIT = 8
 PART = 6
+FIRST = (0, 2, 1, 0, 2, 1, 2, 0, 1, 2, 0, 1)
 UW = UNIT * W
 OC = NR * W // 16
+LC = COLS // 16
 SCALE = COLS // W
-PIECES = ((0, 48), (48, 88), (88, 128))
-PW = 48
-PARTS = (256, 416, 352)
+NP = NR // 2
+BOUNDS = (0, 6, 12, 16, 22, 28, 32)
+STEPS = (1, 2, 1)
+MORE = (1, 1)
 
 SCRATCH = {
     "xs": ("sbuf", [128, COLS], "float32"),
+    "w": ("sbuf", [128, COLS], "float32"),
+    "z": ("sbuf", [128, COLS], "float32"),
     "rx": ("sbuf", [128, UW], "float32"),
     "win": ("sbuf", [128, NR * W], "float32"),
     "wout": ("sbuf", [128, NR * W], "float32"),
-    "z": ("sbuf", [128, COLS], "float32"),
-    "yo": ("sbuf", [128, COLS], "float32"),
     "hraw": ("sbuf", [128, 2], "int32"),
+    "hp": ("sbuf", [128, 3], "int32"),
     "oh": ("sbuf", [128, 128], "float32"),
     "rhs": ("sbuf", [128, 1], "float32"),
     "pi": ("sbuf", [128, 1], "int32"),
+    "pk": ("sbuf", [128, 1], "float32"),
     "pm": ("sbuf", [128, 1], "int32"),
     "pf": ("sbuf", [128, 1], "float32"),
+    "mm": ("sbuf", [128, LC], "int32"),
+    "m4": ("sbuf", [128, LC], "int32"),
     "ia": ("sbuf", [128, OC], "int32"),
     "ib": ("sbuf", [128, OC], "int32"),
-    "ip": ("sbuf", [128, PW], "int32"),
     "ja": ("sbuf", [128, OC], "float32"),
     "jb": ("sbuf", [128, OC], "int32"),
-    "jp": ("sbuf", [128, PW], "float32"),
+    "jp": ("sbuf", [128, LC], "float32"),
     "ua": ("sbuf", [128, OC], "int32"),
     "ub": ("sbuf", [128, OC], "int32"),
     "uc": ("sbuf", [128, OC], "int32"),
     "um": ("sbuf", [128, OC], "int32"),
     "uf": ("sbuf", [128, OC], "float32"),
-    "ic": ("sbuf", [128, PW], "int32"),
-    "id2": ("sbuf", [128, PW], "int32"),
-    "offp": ("sbuf", [128, PW], "uint16"),
-    "off": ("sbuf", [128, COLS // 16], "uint16"),
+    "ic": ("sbuf", [128, LC], "int32"),
+    "id2": ("sbuf", [128, LC], "int32"),
+    "off": ("sbuf", [128, LC], "uint16"),
     "ps": ("psum", [128, 1], "float32"),
 }
-SEMAPHORES = ["hl", "xl0", "xl1", "xl2", "xl3", "ls", "hs", "xr", "da", "za", "lz", "vz", "vo", "vs", "vp", "gk", "ms",
-              "gv0", "gs0", "gv1", "gs1", "gv2", "gs2", "st"]
+SEMAPHORES = ["hl", "xl", "ls", "hs", "hm", "xr", "da", "vz", "vo", "vs", "gk", "ga", "ms", "co", "cj", "ca", "st", "su"]
+SEMAPHORES += ["%s%d" % (a, b) for a in ("za", "gv", "gs") for b in range(NP)]
 
 _PLAN = {}
 
@@ -79,6 +84,7 @@ def _plan(T, topo):
         return place(a) == place(b) or topo.same_plane(a, b)
 
     rot = []
+    second = {}
     for plane in (True, False):
         cand = []
         for key in sorted(chips):
@@ -87,13 +93,12 @@ def _plan(T, topo):
             mate = any(topo.mates(chips[key][0], r) for r in ranks)
             cand.append((not mate, key[1], key[0]))
         cand = sorted(cand)[:UNIT]
-        for half in range(2):
-            for i, (_m, ch, ho) in enumerate(cand):
-                cores = chips[(ho, ch)]
-                for c in cores:
-                    if topo.die(c) == (half + i) % 2 and all(topo.may_write(c, r) for r in ranks):
-                        rot.append(c)
-                        break
+        for _m, ch, ho in cand:
+            for d in (0, 1):
+                own = [c for c in chips[(ho, ch)] if topo.die(c) == d and all(topo.may_write(c, r) for r in ranks)]
+                rot.append(own[0])
+                second[own[0]] = own[1]
+    gate = dict((r, [c for c in second.values() if topo.mates(c, r) and topo.die(c) == topo.die(r)][0]) for r in ranks)
     unit_of = {}
     helpers = {}
     for ri, r in enumerate(ranks):
@@ -106,19 +111,20 @@ def _plan(T, topo):
             unit_of[c] = (ri, u)
         helpers[r] = sorted([c for c in team if c != r], key=lambda c: ((c in rest) == (r in rest), c))
     calls = {}
-    for r in ranks:
+    for ri, r in enumerate(ranks):
         hp = helpers[r]
         for c in hp[:2]:
             u = unit_of[c][1] * UNIT
             calls[c] = [([u + i for i in range(UNIT)], 1)]
         u = unit_of[hp[2]][1] * UNIT
-        calls[hp[2]] = [([u + i for i in range(4)], 2), ([u + i for i in range(4, PART)], 4)]
+        a = u + FIRST[ri]
+        calls[hp[2]] = [([a + i for i in range(4)], 2), ([a + i for i in range(4, PART)], 4)]
         v = unit_of[r][1] * UNIT
-        calls[r] = [([u + i for i in range(PART, UNIT)], 4), ([v + i for i in range(UNIT)], 1)]
+        calls[r] = [([j for j in range(u, u + UNIT) if not a <= j < a + PART], 4), ([v + i for i in range(UNIT)], 1)]
     taken = {}
 
     def place_rotator(j, seen):
-        for r in ranks:
+        for r in sorted(ranks, key=lambda r: len([c for c in helpers[r] if c in taken])):
             for c in helpers[r]:
                 if unit_of[c][1] != j // UNIT or c in seen:
                     continue
@@ -132,18 +138,17 @@ def _plan(T, topo):
         if not place_rotator(j, set()):
             raise ValueError("no way for hh to rotator %d" % j)
     hnext = {}
-    makers = list(rot)
     for c in taken:
         hnext[c] = rot[taken[c]]
-    spare = [c for d in rot for c in chips[place(d)] if c not in rot and all(topo.may_write(c, r) for r in ranks)]
+    cols = dict((hnext[c], [c]) for c in hnext)
     for r in ranks:
         for c in helpers[r]:
             if c not in hnext:
-                d = [d for d in spare if d not in makers and topo.may_write(c, d)][0]
-                hnext[c] = d
-                makers.append(d)
-    _PLAN.update({"ranks": ranks, "rot": rot, "unit_of": unit_of, "calls": calls, "helpers": helpers,
-                  "hnext": hnext, "makers": makers})
+                cols[[d for d in rot if len(cols[d]) == 1 and topo.may_write(c, d)][0]].append(c)
+    for d in rot:
+        cols[d].append(second[d])
+    _PLAN.update({"ranks": ranks, "rot": rot, "second": second, "gate": gate, "unit_of": unit_of, "calls": calls,
+                  "helpers": helpers, "hnext": hnext, "cols": cols})
     return _PLAN
 
 
@@ -164,41 +169,79 @@ def _send_slices(g, core, T, topo, P, ri, slices, ne, buf, first):
     return ne * len(slices)
 
 
-def _second_turn(j):
-    return j % NR
+def _start(j):
+    return [b for b in range(NP) if BOUNDS[b] <= j < BOUNDS[b + 1]][0]
 
 
-def _phase2(j):
-    return [(list(range(0, 8)), 1), (list(range(8, 12)), 2)]
+def _steps():
+    out = []
+    a = 0
+    for n in STEPS + MORE:
+        out.append((a, n, 4 // n))
+        a += n
+    return out
 
 
-def _hh_engines(e, i):
-    return e[4 * i:4 * i + 4]
+def _send_step(g, core, T, topo, P, j, k, buf, o0):
+    first, cnt, ne = _steps()[k]
+    tr = []
+    for i in range(2 * cnt):
+        o = 2 * first + i
+        d = P["ranks"][(2 * _start(j) + o) % NR]
+        e = _bits(topo.mask(core, d))[i * ne:(i + 1) * ne]
+        if k == 0:
+            d = P["gate"][d]
+        a = (o - o0) * W
+        tr.append(_xfer(T, topo, core, d, _or(e), T.sem["za%d" % k], buf[:, a:a + W], T.z[:, j * W:(j + 1) * W]))
+    g.remote_dma_fused(tr, local_sem=T.sem.ls)
+    return 2 * cnt * ne
 
 
-def _unit_engines(e, i, off_chip):
-    return (e[0:8], e[8:16], [b for b in e if b not in off_chip])[i]
+def _relay_engines(topo, P, r):
+    off_chip = _bits(topo.mask(r, P["ranks"][0]))
+    return [b for b in _bits(topo.mask(r, P["second"][r])) if b not in off_chip]
+
+
+def _hh_engines(P, r, c, e):
+    to = [d for d in P["helpers"][r] if d in P["hnext"]]
+    i = to.index(c)
+    if len(to) == 2:
+        return e[8 * i:8 * i + 8]
+    return (e[0:8], e[8:12], e[12:16])[i]
+
+
+def _unit_engines(topo, P, r, i):
+    e = _bits(topo.mask(r, P["helpers"][r][i]))
+    off_chip = _bits(topo.mask(r, P["rot"][P["unit_of"][r][1] * UNIT]))
+    return e if i < 2 else [b for b in e if b not in off_chip]
+
+
+def _columns_mask(topo, P, c, d):
+    return topo.mask(c, P["ranks"][0] if c == P["second"][d] else d)
+
+
+def _columns(g, core, T, topo, P, d):
+    n = NR // len(P["cols"][d])
+    a = P["cols"][d].index(core) * n
+    lo, hi = a * W // 16, (a + n) * W // 16
+    g.iota(T.ia[:, lo:hi], [[0, n], [16, W // 16]], P["rot"].index(d) * W, 0).then_inc(T.sem.gk, 1)
+    g.wait_ge(T.sem.gk, 1)
+    rid, pid = topo.addr(d, core)
+    m = _columns_mask(topo, P, core, d)
+    g.remote_dma(T.ia[:, lo:hi], T.ia[:, lo:hi], T.sem.ca, T.sem.ls, pid, rid, m)
+    return len(_bits(m))
 
 
 def _onehot(g, T):
-    a = T.oh[0:16, :]
+    a = T.oh[:, :]
     g.vector.memset(a, 1.0).then_inc(T.sem.vo, 1)
     g.wait_ge(T.sem.vo, 1)
-    g.affine_select(a, a, [[1, 128]], AluOpType.is_ge, 0.0, 0, -16).then_inc(T.sem.gk, 1)
-    g.wait_ge(T.sem.gk, 1)
-    g.affine_select(a, a, [[-1, 128]], AluOpType.is_ge, 0.0, 15, 16).then_inc(T.sem.gk, 1)
+    g.affine_select(a, a, [[1, 128]], AluOpType.is_ge, 0.0, 0, -16).then_inc(T.sem.ga, 1)
+    g.wait_ge(T.sem.ga, 1)
+    g.affine_select(a, a, [[-1, 128]], AluOpType.is_ge, 0.0, 15, 16).then_inc(T.sem.ga, 1)
 
 
-def _make_lists(g, core, T, topo, P, j):
-    op = AluOpType
-    v = g.vector
-    m = P["makers"].index(core)
-    d = P["ranks"][m // len(PIECES)]
-    lo, hi = PIECES[m % len(PIECES)]
-    pw = hi - lo
-    src = [c for c in P["hnext"] if P["hnext"][c] == core][0]
-    nh = len(_bits(topo.mask(src, core)))
-    rotator = j is not None
+def _counted(T, v):
     n = [0]
 
     def inc(ins):
@@ -208,58 +251,60 @@ def _make_lists(g, core, T, topo, P, j):
     def sync():
         v.wait_ge(T.sem.vs, n[0])
 
-    _onehot(g, T)
-    g.iota(T.pi[:, 0:1], [[0, 1]], 0, 1).then_inc(T.sem.gk, 1)
-    g.iota(T.ip[:, 0:pw], [[16, pw]], 16 * lo, 0).then_inc(T.sem.gk, 1)
-    gk = 4
-    if rotator:
-        t0 = _second_turn(j)
-        g.iota(T.ia[:, :], [[0, NR], [-16, W // 16]], COLS - 1 - j * W, 0).then_inc(T.sem.gk, 1)
+    return n, inc, sync
+
+
+def _rotator_list(g, core, T, topo, P, j):
+    op = AluOpType
+    v = g.vector
+    even = j % 2 == 0
+    mate = P["rot"][j + 1 if even else j - 1]
+    rid, pid = topo.addr(mate, core)
+    m = topo.mask(core, mate)
+    nm = len(_bits(m))
+    n, inc, sync = _counted(T, v)
+    if even:
+        _onehot(g, T)
+        g.wait_ge(T.sem.ga, 2)
+        g.tensor.wait_ge(T.sem.ga, 2)
+        g.remote_dma(T.oh[:, :], T.oh[:, :], T.sem.co, T.sem.ls, pid, rid, m)
+        v.wait_ge(T.sem.cj, nm)
+    else:
+        t0 = 2 * _start(j)
         cut = (NR - t0) * (W // 16)
         g.iota(T.ib[:, 0:cut], [[W, NR - t0], [16, W // 16]], t0 * W, 0).then_inc(T.sem.gk, 1)
-        gk += 2
+        gk = 1
         if t0:
             g.iota(T.ib[:, cut:OC], [[W, t0], [16, W // 16]], 0, 0).then_inc(T.sem.gk, 1)
-            gk += 1
-    v.wait_ge(T.sem.gk, gk)
-    inc(v.tensor_scalar(T.pm[:, 0:1], T.pi[:, 0:1], 15, None, op.bitwise_and))
-    sync()
-    inc(v.tensor_copy(T.pf[:, 0:1], T.pm[:, 0:1]))
-    sync()
-    if rotator:
-        inc(v.tensor_scalar(T.ja[:, :], T.ia[:, :], T.pf[:, 0:1], None, op.subtract))
-        inc(v.tensor_scalar(T.jb[:, :], T.ib[:, :], T.pf[:, 0:1], float(SCALE), op.add, op.mult))
-    inc(v.tensor_scalar(T.jp[:, 0:pw], T.ip[:, 0:pw], T.pf[:, 0:1], None, op.add))
-    sync()
-    v.wait_ge(T.sem.hs, nh)
-    inc(v.tensor_copy(T.rhs[0:16, 0:1], T.hraw[0:16, 0:1]))
+            gk = 2
+        g.wait_ge(T.sem.gk, gk)
+        g.remote_dma(T.ib[:, :], T.ib[:, :], T.sem.cj, T.sem.ls, pid, rid, m)
+        g.tensor.wait_ge(T.sem.co, nm)
+        v.wait_ge(T.sem.gk, gk)
+    src = P["cols"][core][0]
+    v.wait_ge(T.sem.ca, sum(len(_bits(_columns_mask(topo, P, c, core))) for c in P["cols"][core]))
+    v.wait_ge(T.sem.hs, len(_bits(topo.mask(src, core))))
+    inc(v.tensor_copy(T.rhs[0:16, 0:1], T.hp[0:16, 0:1]))
     g.tensor.wait_ge(T.sem.vs, n[0])
     g.tensor.matmul(T.ps[:, 0:1], T.oh[0:16, :], T.rhs[0:16, 0:1], True, True).then_inc(T.sem.ms, 1)
+    inc(v.tensor_copy(T.pf[:, 0:1], T.hp[:, 2:3]))
+    sync()
+    inc(v.tensor_scalar(T.ja[:, :], T.ia[:, :], T.pf[:, 0:1], None, op.add))
+    inc(v.tensor_scalar(T.jb[:, :], T.ib[:, :], T.pf[:, 0:1], float(SCALE), op.add, op.mult))
+    sync()
     v.wait_ge(T.sem.ms, 1)
-    v.tensor_scalar(T.ic[:, 0:pw], T.jp[:, 0:pw], T.ps[:, 0:1], None, op.add).then_inc(T.sem.vp, 1)
-    if rotator:
-        inc(v.tensor_scalar(T.ua[:, :], T.ja[:, :], T.ps[:, 0:1], None, op.add))
-    v.wait_ge(T.sem.vp, 1)
-    v.tensor_scalar(T.id2[:, 0:pw], T.ic[:, 0:pw], COLS - 1, None, op.bitwise_and).then_inc(T.sem.vp, 1)
-    if rotator:
-        sync()
-        inc(v.tensor_scalar(T.ub[:, :], T.ua[:, :], 15 * COLS, None, op.bitwise_and))
-    v.wait_ge(T.sem.vp, 2)
-    v.tensor_copy(T.offp[:, 0:pw], T.id2[:, 0:pw]).then_inc(T.sem.vp, 1)
-    if rotator:
-        sync()
-        inc(v.tensor_tensor(T.uc[:, :], T.ub[:, :], T.jb[:, :], op.add))
-        sync()
-        inc(v.tensor_scalar(T.um[:, :], T.uc[:, :], float(NR * COLS), float(-NR * COLS), op.is_ge, op.mult))
-        sync()
-        inc(v.tensor_tensor(T.uf[:, :], T.uc[:, :], T.um[:, :], op.add))
-        sync()
-        inc(v.tensor_scalar(T.off[:, 0:OC], T.uf[:, :], 1.0 / SCALE, None, op.mult))
-    g.wait_ge(T.sem.vp, 3)
-    rid, pid = topo.addr(d, core)
-    e = topo.mask(core, d)
-    g.remote_dma(T.off[:, lo:hi], T.offp[:, 0:pw], T.sem.lz, T.sem.ls, pid, rid, e)
-    return n[0], len(_bits(e))
+    inc(v.tensor_scalar(T.ua[:, :], T.ja[:, :], T.ps[:, 0:1], None, op.add))
+    sync()
+    inc(v.tensor_scalar(T.ub[:, :], T.ua[:, :], 15 * COLS, None, op.bitwise_and))
+    sync()
+    inc(v.tensor_tensor(T.uc[:, :], T.ub[:, :], T.jb[:, :], op.add))
+    sync()
+    inc(v.tensor_scalar(T.um[:, :], T.uc[:, :], float(NR * COLS), float(-NR * COLS), op.is_ge, op.mult))
+    sync()
+    inc(v.tensor_tensor(T.uf[:, :], T.uc[:, :], T.um[:, :], op.add))
+    sync()
+    inc(v.tensor_scalar(T.off[:, 0:OC], T.uf[:, :], 1.0 / SCALE, None, op.mult))
+    return n[0], nm
 
 
 def _turn(queue, is_vector, out, win, off, sem):
@@ -269,119 +314,172 @@ def _turn(queue, is_vector, out, win, off, sem):
         queue.activation(out, win.indirect(off), ActivationFunctionType.Copy).then_inc(sem, 1)
 
 
-def _off_chip(topo, P, r):
-    return _bits(topo.mask(r, P["rot"][P["unit_of"][r][1] * UNIT]))
-
-
 def _rank(g, core, T, topo, P):
+    op = AluOpType
+    v = g.vector
     ri = P["ranks"].index(core)
     hp = P["helpers"][core]
-    g.vector.memset(T.hraw[32:64, :], 0).then_inc(T.sem.vz, 1)
-    g.vector.memset(T.hraw[64:128, :], 0).then_inc(T.sem.vz, 1)
-    units = [P["unit_of"][c][1] for c in hp + [core]]
     g.sync.dma_start(T.hraw[0:16, :], T.hh[:, :]).then_inc(T.sem.hl, 16)
     g.scalar.dma_start(T.hraw[16:32, :], T.hh[:, :]).then_inc(T.sem.hl, 16)
-    for i, u in enumerate(units):
-        q = g.scalar if i % 2 == 0 else g.sync
-        q.dma_start(T.xs[:, u * UW:(u + 1) * UW], T.x[:, u * UW:(u + 1) * UW]).then_inc(T.sem["xl%d" % i], 16)
-    ls = 0
-    tr = []
+    h = COLS // 2
+    g.sync.dma_start(T.xs[:, 0:h], T.x[:, 0:h]).then_inc(T.sem.xl, 16)
+    g.scalar.dma_start(T.xs[:, h:COLS], T.x[:, h:COLS]).then_inc(T.sem.xl, 16)
+    n, inc, sync = _counted(T, v)
+    g.iota(T.pi[:, 0:1], [[0, 1]], 0, 1).then_inc(T.sem.gk, 1)
+    g.iota(T.mm[:, :], [[1, LC]], 0, 0).then_inc(T.sem.ga, 1)
+    v.wait_ge(T.sem.gk, 1)
+    inc(v.tensor_scalar(T.pm[:, 0:1], T.pi[:, 0:1], 15, None, op.bitwise_and))
+    sync()
+    g.wait_ge(T.sem.vs, 1)
+    to = [c for c in hp if c in P["hnext"]]
+    eng = dict((c, _hh_engines(P, core, c, _bits(topo.mask(core, c)))) for c in to)
+    g.remote_dma_fused([_xfer(T, topo, core, c, _or(eng[c]), T.sem.hm, T.pm[:, 0:1], T.hp[:, 2:3]) for c in to],
+                       local_sem=T.sem.ls)
+    inc(v.tensor_copy(T.pk[:, 0:1], T.pi[:, 0:1]))
+    v.memset(T.hraw[32:64, :], 0).then_inc(T.sem.vz, 1)
+    v.memset(T.hraw[64:128, :], 0).then_inc(T.sem.vz, 1)
+    v.wait_ge(T.sem.ga, 1)
+    inc(v.tensor_scalar(T.m4[:, :], T.mm[:, :], 4, None, op.arith_shift_right))
+    inc(v.tensor_copy(T.pf[:, 0:1], T.pm[:, 0:1]))
+    sync()
+    inc(v.tensor_scalar(T.oh[:, :], T.m4[:, :], T.pk[:, 0:1], None, op.is_equal))
+    inc(v.tensor_scalar(T.jp[:, :], T.mm[:, :], 16.0, T.pf[:, 0:1], op.mult, op.add))
+    sync()
     g.wait_ge(T.sem.vz, 2)
     g.wait_ge(T.sem.hl, 32)
-    for i, c in enumerate(hp):
-        e = _hh_engines(_bits(topo.mask(core, c)), i)
-        tr.append(_xfer(T, topo, core, c, _or(e), T.sem.hs, T.hraw[:, :], T.hraw[:, :]))
-        ls += len(e)
-    g.remote_dma_fused(tr, local_sem=T.sem.ls)
-    for group in ((0, 1), (2,)):
-        tr = []
-        for i in group:
-            g.wait_ge(T.sem["xl%d" % i], 16)
-            w = UW if i < 2 else PART * W
-            e = _unit_engines(_bits(topo.mask(core, hp[i])), i, _off_chip(topo, P, core))
-            tr.append(_xfer(T, topo, core, hp[i], _or(e), T.sem.xr,
-                            T.xs[:, units[i] * UW:units[i] * UW + w], T.rx[:, 0:w]))
-            ls += len(e)
-        g.remote_dma_fused(tr, local_sem=T.sem.ls)
-    for k, (slices, ne) in enumerate(P["calls"][core]):
-        if k:
-            g.wait_ge(T.sem.xl3, 16)
-        ls += _send_slices(g, core, T, topo, P, ri, slices, ne, T.xs, 0)
-    za = 0
-    for j in range(J):
-        for slots, ne in _phase2(j):
-            for o in slots:
-                if (_second_turn(j) + o) % NR == ri:
-                    za += ne
-    lz = 0
-    for m, c in enumerate(P["makers"]):
-        if m // len(PIECES) == ri:
-            lz += len(_bits(topo.mask(c, core)))
-    for k, (queue, isv) in enumerate(((g.vector, True), (g.scalar, False))):
-        queue.wait_ge(T.sem.lz, lz)
-        queue.wait_ge(T.sem.za, za)
-        a = 0
-        for i, w in enumerate(PARTS):
-            lo = a + k * w
-            _turn(queue, isv, T.yo[:, lo:lo + w], T.z[:, :], T.off[:, lo // 16:(lo + w) // 16],
+    g.remote_dma_fused([_xfer(T, topo, core, c, _or(eng[c]), T.sem.hs, T.hraw[:, :], T.hp[:, 0:2]) for c in to],
+                       local_sem=T.sem.ls)
+    ls = 2 * sum(len(eng[c]) for c in to)
+    v.wait_ge(T.sem.hl, 32)
+    inc(v.tensor_copy(T.rhs[0:16, 0:1], T.hraw[0:16, 0:1]))
+    g.tensor.wait_ge(T.sem.vs, n[0])
+    g.tensor.matmul(T.ps[:, 0:1], T.oh[0:16, :], T.rhs[0:16, 0:1], True, True).then_inc(T.sem.ms, 1)
+    v.wait_ge(T.sem.ms, 1)
+    inc(v.tensor_scalar(T.ic[:, :], T.jp[:, :], T.ps[:, 0:1], None, op.add))
+    sync()
+    inc(v.tensor_scalar(T.id2[:, :], T.ic[:, :], COLS - 1, None, op.bitwise_and))
+    sync()
+    inc(v.tensor_copy(T.off[:, :], T.id2[:, :]))
+    units = [P["unit_of"][c][1] for c in hp + [core]]
+    a, b = P["calls"][core][0][0]
+    parts = [(u * UW, u * UW + UW // 2, UW // 2) for u in units]
+    lo = P["calls"][hp[2]][0][0][0] * W
+    parts[2:3] = [(lo, lo + PART * W // 2, PART * W // 2), (a * W, b * W, W)]
+    for k, (queue, isv) in enumerate(((v, True), (g.scalar, False))):
+        queue.wait_ge(T.sem.vs, n[0])
+        queue.wait_ge(T.sem.xl, 32)
+        for i, pt in enumerate(parts):
+            lo = pt[k]
+            hi = lo + pt[2]
+            _turn(queue, isv, T.w[:, lo:hi], T.xs[:, :], T.off[:, lo // 16:hi // 16],
                   T.sem[("gv%d" if isv else "gs%d") % i])
-            a += 2 * w
-    a = 0
-    for i, w in enumerate(PARTS):
-        g.sync.wait_ge(T.sem["gv%d" % i], 1)
-        g.sync.wait_ge(T.sem["gs%d" % i], 1)
-        g.sync.dma_start(T.y[:, a:a + 2 * w], T.yo[:, a:a + 2 * w]).then_inc(T.sem.st, 16)
-        a += 2 * w
-    g.sync.wait_ge(T.sem.st, 16 * len(PARTS))
+
+    def turned(i):
+        g.wait_ge(T.sem["gv%d" % i], 1)
+        g.wait_ge(T.sem["gs%d" % i], 1)
+
+    for i in range(3):
+        turned(i)
+        lo, wd = parts[i][0], 2 * parts[i][2]
+        e = _unit_engines(topo, P, core, i)
+        rid, pid = topo.addr(hp[i], core)
+        g.remote_dma(T.rx[:, 0:wd], T.w[:, lo:lo + wd], T.sem.xr, T.sem.ls, pid, rid, _or(e))
+        ls += len(e)
+    for k, (slices, ne) in enumerate(P["calls"][core]):
+        turned(3 + k)
+        ls += _send_slices(g, core, T, topo, P, ri, slices, ne, T.w, 0)
+    for q, sem, ks in ((g.sync, T.sem.st, (1, 0, 2)), (g.scalar, T.sem.su, (3, 4))):
+        stores = 0
+        for k in ks:
+            first, cnt, ne = _steps()[k]
+            blocks = sorted((ri // 2 - first - i) % NP for i in range(cnt))
+            need = sum(ne * (BOUNDS[b + 1] - BOUNDS[b]) for b in blocks)
+            if k == 0:
+                need = len(_bits(topo.mask(P["gate"][core], core)))
+            q.wait_ge(T.sem["za%d" % k], need)
+            runs = [[blocks[0], blocks[0] + 1]]
+            for b in blocks[1:]:
+                if b == runs[-1][1]:
+                    runs[-1][1] = b + 1
+                else:
+                    runs.append([b, b + 1])
+            for b0, b1 in runs:
+                lo, hi = BOUNDS[b0] * W, BOUNDS[b1] * W
+                q.dma_start(T.y[:, lo:hi], T.z[:, lo:hi]).then_inc(sem, 16)
+                stores += 1
+        q.wait_ge(sem, 16 * stores)
     g.wait_ge(T.sem.ls, ls)
 
 
 def _helper(g, core, T, topo, P):
-    ri, unit = P["unit_of"][core]
+    ri = P["unit_of"][core][0]
     r = P["ranks"][ri]
     i = P["helpers"][r].index(core)
-    d = P["hnext"][core]
-    rid, pid = topo.addr(d, core)
-    m = topo.mask(core, d)
-    g.wait_ge(T.sem.hs, len(_hh_engines(_bits(topo.mask(r, core)), i)))
-    g.remote_dma(T.hraw[:, :], T.hraw[:, :], T.sem.hs, T.sem.ls, pid, rid, m)
-    ls = len(_bits(m))
-    g.wait_ge(T.sem.xr, len(_unit_engines(_bits(topo.mask(r, core)), i, _off_chip(topo, P, r))))
+    d = [c for c in P["cols"] if core in P["cols"][c]][0]
+    ls = _columns(g, core, T, topo, P, d)
+    if core in P["hnext"]:
+        e = len(_hh_engines(P, r, core, _bits(topo.mask(r, core))))
+        g.wait_ge(T.sem.hm, e)
+        g.wait_ge(T.sem.hs, e)
+        rid, pid = topo.addr(d, core)
+        m = topo.mask(core, d)
+        g.remote_dma(T.hp[:, :], T.hp[:, :], T.sem.hs, T.sem.ls, pid, rid, m)
+        ls += len(_bits(m))
+    g.wait_ge(T.sem.xr, len(_unit_engines(topo, P, r, i)))
+    first = P["calls"][core][0][0][0]
     for slices, ne in P["calls"][core]:
-        ls += _send_slices(g, core, T, topo, P, ri, slices, ne, T.rx, unit * UNIT)
-    g.wait_ge(T.sem.ls, ls)
-
-
-def _maker(g, core, T, topo, P):
-    _nv, ls = _make_lists(g, core, T, topo, P, None)
+        ls += _send_slices(g, core, T, topo, P, ri, slices, ne, T.rx, first)
     g.wait_ge(T.sem.ls, ls)
 
 
 def _rotator(g, core, T, topo, P):
     j = P["rot"].index(core)
-    t0 = _second_turn(j)
-    nv, ls = _make_lists(g, core, T, topo, P, j)
+    nv, ls = _rotator_list(g, core, T, topo, P, j)
     da = 0
     for c in P["calls"]:
         for slices, ne in P["calls"][c]:
             if j in slices:
                 da += ne
-    for queue, isv in ((g.vector, True), (g.scalar, False)):
+    o0 = 2 * sum(STEPS)
+    parts = [(2 * first, 2 * cnt) for first, cnt, _ne in _steps()[:len(STEPS)]]
+    parts.insert(1, (o0, NR - o0))
+    for k, (queue, isv) in enumerate(((g.vector, True), (g.scalar, False))):
         queue.wait_ge(T.sem.vs, nv)
         queue.wait_ge(T.sem.da, da)
-        parts = ((0, 4, "gv1"), (8, 10, "gv2")) if isv else ((4, 8, "gs1"), (10, 12, "gs2"))
-        for a, b, nm in parts:
-            _turn(queue, isv, T.wout[:, a * W:b * W], T.win[:, :], T.off[:, a * W // 16:b * W // 16], T.sem[nm])
-    for k, (slots, ne) in enumerate(_phase2(j)):
-        g.wait_ge(T.sem["gv%d" % (k + 1)], 1)
-        g.wait_ge(T.sem["gs%d" % (k + 1)], 1)
-        tr = []
-        for i, o in enumerate(slots):
-            d = P["ranks"][(t0 + o) % NR]
-            e = _bits(topo.mask(core, d))[i * ne:(i + 1) * ne]
-            tr.append(_xfer(T, topo, core, d, _or(e), T.sem.za, T.wout[:, o * W:(o + 1) * W], T.z[:, j * W:(j + 1) * W]))
-            ls += ne
-        g.remote_dma_fused(tr, local_sem=T.sem.ls)
+        for i, (o, cnt) in enumerate(parts):
+            a = o + k * cnt // 2
+            b = a + cnt // 2
+            _turn(queue, isv, T.wout[:, a * W:b * W], T.win[:, :], T.off[:, a * W // 16:b * W // 16],
+                  T.sem[("gv%d" if isv else "gs%d") % i])
+    for i in range(len(parts)):
+        g.wait_ge(T.sem["gv%d" % i], 1)
+        g.wait_ge(T.sem["gs%d" % i], 1)
+        if i == 1:
+            d = P["second"][core]
+            e = _relay_engines(topo, P, core)
+            rid, pid = topo.addr(d, core)
+            g.remote_dma(T.rx[:, 0:(NR - o0) * W], T.wout[:, o0 * W:NR * W], T.sem.xr, T.sem.ls, pid, rid, _or(e))
+            ls += len(e)
+        else:
+            ls += _send_step(g, core, T, topo, P, j, i - (i > 1), T.wout, 0)
+    g.wait_ge(T.sem.ls, ls)
+
+
+def _second(g, core, T, topo, P):
+    r = [c for c in P["rot"] if P["second"][c] == core][0]
+    ls = _columns(g, core, T, topo, P, r)
+    g.wait_ge(T.sem.xr, len(_relay_engines(topo, P, r)))
+    for k in range(len(MORE)):
+        ls += _send_step(g, core, T, topo, P, P["rot"].index(r), len(STEPS) + k, T.rx, 2 * sum(STEPS))
+    for ri, d in enumerate(P["ranks"]):
+        if P["gate"][d] == core:
+            b = ri // 2
+            g.wait_ge(T.sem.za0, _steps()[0][2] * (BOUNDS[b + 1] - BOUNDS[b]))
+            lo, hi = BOUNDS[b] * W, BOUNDS[b + 1] * W
+            rid, pid = topo.addr(d, core)
+            m = topo.mask(core, d)
+            g.remote_dma(T.z[:, lo:hi], T.z[:, lo:hi], T.sem.za0, T.sem.ls, pid, rid, m)
+            ls += len(_bits(m))
     g.wait_ge(T.sem.ls, ls)
 
 
@@ -393,5 +491,5 @@ def rank_program(g, core, T, topo):
         _helper(g, core, T, topo, P)
     elif core in P["rot"]:
         _rotator(g, core, T, topo, P)
-    elif core in P["makers"]:
-        _maker(g, core, T, topo, P)
+    elif core in P["second"].values():
+        _second(g, core, T, topo, P)

from concourse.bass import DstId, RemoteDMATransfer
from concourse.mybir import AluOpType, ActivationFunctionType

SIM = 256
COLS = 2048
NR = 12
J = 32
W = COLS // J
UNIT = 8
PART = 6
FIRST = (0, 2, 1, 0, 2, 1, 2, 0, 1, 2, 0, 1)
UW = UNIT * W
OC = NR * W // 16
LC = COLS // 16
SCALE = COLS // W
NP = NR // 2
BOUNDS = (0, 6, 12, 16, 22, 28, 32)
STEPS = (1, 2, 1)
MORE = (1, 1)

SCRATCH = {
    "xs": ("sbuf", [128, COLS], "float32"),
    "w": ("sbuf", [128, COLS], "float32"),
    "z": ("sbuf", [128, COLS], "float32"),
    "rx": ("sbuf", [128, UW], "float32"),
    "win": ("sbuf", [128, NR * W], "float32"),
    "wout": ("sbuf", [128, NR * W], "float32"),
    "hraw": ("sbuf", [128, 2], "int32"),
    "hp": ("sbuf", [128, 3], "int32"),
    "oh": ("sbuf", [128, 128], "float32"),
    "rhs": ("sbuf", [128, 1], "float32"),
    "pi": ("sbuf", [128, 1], "int32"),
    "pk": ("sbuf", [128, 1], "float32"),
    "pm": ("sbuf", [128, 1], "int32"),
    "pf": ("sbuf", [128, 1], "float32"),
    "mm": ("sbuf", [128, LC], "int32"),
    "m4": ("sbuf", [128, LC], "int32"),
    "ia": ("sbuf", [128, OC], "int32"),
    "ib": ("sbuf", [128, OC], "int32"),
    "ja": ("sbuf", [128, OC], "float32"),
    "jb": ("sbuf", [128, OC], "int32"),
    "jp": ("sbuf", [128, LC], "float32"),
    "ua": ("sbuf", [128, OC], "int32"),
    "ub": ("sbuf", [128, OC], "int32"),
    "uc": ("sbuf", [128, OC], "int32"),
    "um": ("sbuf", [128, OC], "int32"),
    "uf": ("sbuf", [128, OC], "float32"),
    "ic": ("sbuf", [128, LC], "int32"),
    "id2": ("sbuf", [128, LC], "int32"),
    "off": ("sbuf", [128, LC], "uint16"),
    "ps": ("psum", [128, 1], "float32"),
}
SEMAPHORES = ["hl", "xl", "ls", "hs", "hm", "xr", "da", "vz", "vo", "vs", "gk", "ga", "ms", "co", "cj", "ca", "st", "su"]
SEMAPHORES += ["%s%d" % (a, b) for a in ("za", "gv", "gs") for b in range(NP)]

_PLAN = {}


def _bits(mask):
    return [1 << b for b in range(mask.bit_length()) if (mask >> b) & 1]


def _or(bits):
    m = 0
    for b in bits:
        m |= b
    return m


def _plan(T, topo):
    if _PLAN:
        return _PLAN
    ranks = [int(c) for c in T.cores]

    def place(c):
        return (topo.host(c), topo.chip(c))

    chips = {}
    for c in range(SIM):
        chips.setdefault(place(c), []).append(c)
    rank_chips = set(place(c) for c in ranks)

    def own_plane(a, b):
        return place(a) == place(b) or topo.same_plane(a, b)

    rot = []
    second = {}
    for plane in (True, False):
        cand = []
        for key in sorted(chips):
            if key in rank_chips or own_plane(chips[key][0], ranks[0]) != plane:
                continue
            mate = any(topo.mates(chips[key][0], r) for r in ranks)
            cand.append((not mate, key[1], key[0]))
        cand = sorted(cand)[:UNIT]
        for _m, ch, ho in cand:
            for d in (0, 1):
                own = [c for c in chips[(ho, ch)] if topo.die(c) == d and all(topo.may_write(c, r) for r in ranks)]
                rot.append(own[0])
                second[own[0]] = own[1]
    gate = dict((r, [c for c in second.values() if topo.mates(c, r) and topo.die(c) == topo.die(r)][0]) for r in ranks)
    unit_of = {}
    helpers = {}
    for ri, r in enumerate(ranks):
        team = [c for c in chips[place(r)] if topo.die(c) == topo.die(r)]
        reach_all = [c for c in team if all(topo.may_write(c, d) for d in rot)]
        rest = [c for c in team if c not in reach_all]
        near = [u for u in range(J // UNIT) if own_plane(rot[u * UNIT], r)]
        far = [u for u in range(J // UNIT) if u not in near]
        for c, u in list(zip(rest, near)) + list(zip(reach_all, far)):
            unit_of[c] = (ri, u)
        helpers[r] = sorted([c for c in team if c != r], key=lambda c: ((c in rest) == (r in rest), c))
    calls = {}
    for ri, r in enumerate(ranks):
        hp = helpers[r]
        for c in hp[:2]:
            u = unit_of[c][1] * UNIT
            calls[c] = [([u + i for i in range(UNIT)], 1)]
        u = unit_of[hp[2]][1] * UNIT
        a = u + FIRST[ri]
        calls[hp[2]] = [([a + i for i in range(4)], 2), ([a + i for i in range(4, PART)], 4)]
        v = unit_of[r][1] * UNIT
        calls[r] = [([j for j in range(u, u + UNIT) if not a <= j < a + PART], 4), ([v + i for i in range(UNIT)], 1)]
    taken = {}

    def place_rotator(j, seen):
        for r in sorted(ranks, key=lambda r: len([c for c in helpers[r] if c in taken])):
            for c in helpers[r]:
                if unit_of[c][1] != j // UNIT or c in seen:
                    continue
                seen.add(c)
                if c not in taken or place_rotator(taken[c], seen):
                    taken[c] = j
                    return True
        return False

    for j in range(J):
        if not place_rotator(j, set()):
            raise ValueError("no way for hh to rotator %d" % j)
    hnext = {}
    for c in taken:
        hnext[c] = rot[taken[c]]
    cols = dict((hnext[c], [c]) for c in hnext)
    for r in ranks:
        for c in helpers[r]:
            if c not in hnext:
                cols[[d for d in rot if len(cols[d]) == 1 and topo.may_write(c, d)][0]].append(c)
    for d in rot:
        cols[d].append(second[d])
    _PLAN.update({"ranks": ranks, "rot": rot, "second": second, "gate": gate, "unit_of": unit_of, "calls": calls,
                  "helpers": helpers, "hnext": hnext, "cols": cols})
    return _PLAN


def _xfer(T, topo, src_core, dst_core, mask, sem, src, dst):
    rid, pid = topo.addr(dst_core, src_core)
    return RemoteDMATransfer(dst_ids=[DstId(rid=rid, pnc=pid)], dma_engine_mask=mask, remote_sem=sem,
                             srcs=[src], dsts=[dst])


def _send_slices(g, core, T, topo, P, ri, slices, ne, buf, first):
    tr = []
    for i, j in enumerate(slices):
        d = P["rot"][j]
        e = _bits(topo.mask(core, d))[i * ne:(i + 1) * ne]
        a = (j - first) * W
        tr.append(_xfer(T, topo, core, d, _or(e), T.sem.da, buf[:, a:a + W], T.win[:, ri * W:(ri + 1) * W]))
    g.remote_dma_fused(tr, local_sem=T.sem.ls)
    return ne * len(slices)


def _start(j):
    return [b for b in range(NP) if BOUNDS[b] <= j < BOUNDS[b + 1]][0]


def _steps():
    out = []
    a = 0
    for n in STEPS + MORE:
        out.append((a, n, 4 // n))
        a += n
    return out


def _send_step(g, core, T, topo, P, j, k, buf, o0):
    first, cnt, ne = _steps()[k]
    tr = []
    for i in range(2 * cnt):
        o = 2 * first + i
        d = P["ranks"][(2 * _start(j) + o) % NR]
        e = _bits(topo.mask(core, d))[i * ne:(i + 1) * ne]
        if k == 0:
            d = P["gate"][d]
        a = (o - o0) * W
        tr.append(_xfer(T, topo, core, d, _or(e), T.sem["za%d" % k], buf[:, a:a + W], T.z[:, j * W:(j + 1) * W]))
    g.remote_dma_fused(tr, local_sem=T.sem.ls)
    return 2 * cnt * ne


def _relay_engines(topo, P, r):
    off_chip = _bits(topo.mask(r, P["ranks"][0]))
    return [b for b in _bits(topo.mask(r, P["second"][r])) if b not in off_chip]


def _hh_engines(P, r, c, e):
    to = [d for d in P["helpers"][r] if d in P["hnext"]]
    i = to.index(c)
    if len(to) == 2:
        return e[8 * i:8 * i + 8]
    return (e[0:8], e[8:12], e[12:16])[i]


def _unit_engines(topo, P, r, i):
    e = _bits(topo.mask(r, P["helpers"][r][i]))
    off_chip = _bits(topo.mask(r, P["rot"][P["unit_of"][r][1] * UNIT]))
    return e if i < 2 else [b for b in e if b not in off_chip]


def _columns_mask(topo, P, c, d):
    return topo.mask(c, P["ranks"][0] if c == P["second"][d] else d)


def _columns(g, core, T, topo, P, d):
    n = NR // len(P["cols"][d])
    a = P["cols"][d].index(core) * n
    lo, hi = a * W // 16, (a + n) * W // 16
    g.iota(T.ia[:, lo:hi], [[0, n], [16, W // 16]], P["rot"].index(d) * W, 0).then_inc(T.sem.gk, 1)
    g.wait_ge(T.sem.gk, 1)
    rid, pid = topo.addr(d, core)
    m = _columns_mask(topo, P, core, d)
    g.remote_dma(T.ia[:, lo:hi], T.ia[:, lo:hi], T.sem.ca, T.sem.ls, pid, rid, m)
    return len(_bits(m))


def _onehot(g, T):
    a = T.oh[:, :]
    g.vector.memset(a, 1.0).then_inc(T.sem.vo, 1)
    g.wait_ge(T.sem.vo, 1)
    g.affine_select(a, a, [[1, 128]], AluOpType.is_ge, 0.0, 0, -16).then_inc(T.sem.ga, 1)
    g.wait_ge(T.sem.ga, 1)
    g.affine_select(a, a, [[-1, 128]], AluOpType.is_ge, 0.0, 15, 16).then_inc(T.sem.ga, 1)


def _counted(T, v):
    n = [0]

    def inc(ins):
        ins.then_inc(T.sem.vs, 1)
        n[0] += 1

    def sync():
        v.wait_ge(T.sem.vs, n[0])

    return n, inc, sync


def _rotator_list(g, core, T, topo, P, j):
    op = AluOpType
    v = g.vector
    even = j % 2 == 0
    mate = P["rot"][j + 1 if even else j - 1]
    rid, pid = topo.addr(mate, core)
    m = topo.mask(core, mate)
    nm = len(_bits(m))
    n, inc, sync = _counted(T, v)
    if even:
        _onehot(g, T)
        g.wait_ge(T.sem.ga, 2)
        g.tensor.wait_ge(T.sem.ga, 2)
        g.remote_dma(T.oh[:, :], T.oh[:, :], T.sem.co, T.sem.ls, pid, rid, m)
        v.wait_ge(T.sem.cj, nm)
    else:
        t0 = 2 * _start(j)
        cut = (NR - t0) * (W // 16)
        g.iota(T.ib[:, 0:cut], [[W, NR - t0], [16, W // 16]], t0 * W, 0).then_inc(T.sem.gk, 1)
        gk = 1
        if t0:
            g.iota(T.ib[:, cut:OC], [[W, t0], [16, W // 16]], 0, 0).then_inc(T.sem.gk, 1)
            gk = 2
        g.wait_ge(T.sem.gk, gk)
        g.remote_dma(T.ib[:, :], T.ib[:, :], T.sem.cj, T.sem.ls, pid, rid, m)
        g.tensor.wait_ge(T.sem.co, nm)
        v.wait_ge(T.sem.gk, gk)
    src = P["cols"][core][0]
    v.wait_ge(T.sem.ca, sum(len(_bits(_columns_mask(topo, P, c, core))) for c in P["cols"][core]))
    v.wait_ge(T.sem.hs, len(_bits(topo.mask(src, core))))
    inc(v.tensor_copy(T.rhs[0:16, 0:1], T.hp[0:16, 0:1]))
    g.tensor.wait_ge(T.sem.vs, n[0])
    g.tensor.matmul(T.ps[:, 0:1], T.oh[0:16, :], T.rhs[0:16, 0:1], True, True).then_inc(T.sem.ms, 1)
    inc(v.tensor_copy(T.pf[:, 0:1], T.hp[:, 2:3]))
    sync()
    inc(v.tensor_scalar(T.ja[:, :], T.ia[:, :], T.pf[:, 0:1], None, op.add))
    inc(v.tensor_scalar(T.jb[:, :], T.ib[:, :], T.pf[:, 0:1], float(SCALE), op.add, op.mult))
    sync()
    v.wait_ge(T.sem.ms, 1)
    inc(v.tensor_scalar(T.ua[:, :], T.ja[:, :], T.ps[:, 0:1], None, op.add))
    sync()
    inc(v.tensor_scalar(T.ub[:, :], T.ua[:, :], 15 * COLS, None, op.bitwise_and))
    sync()
    inc(v.tensor_tensor(T.uc[:, :], T.ub[:, :], T.jb[:, :], op.add))
    sync()
    inc(v.tensor_scalar(T.um[:, :], T.uc[:, :], float(NR * COLS), float(-NR * COLS), op.is_ge, op.mult))
    sync()
    inc(v.tensor_tensor(T.uf[:, :], T.uc[:, :], T.um[:, :], op.add))
    sync()
    inc(v.tensor_scalar(T.off[:, 0:OC], T.uf[:, :], 1.0 / SCALE, None, op.mult))
    return n[0], nm


def _turn(queue, is_vector, out, win, off, sem):
    if is_vector:
        queue.tensor_copy(out, win.indirect(off)).then_inc(sem, 1)
    else:
        queue.activation(out, win.indirect(off), ActivationFunctionType.Copy).then_inc(sem, 1)


def _rank(g, core, T, topo, P):
    op = AluOpType
    v = g.vector
    ri = P["ranks"].index(core)
    hp = P["helpers"][core]
    g.sync.dma_start(T.hraw[0:16, :], T.hh[:, :]).then_inc(T.sem.hl, 16)
    g.scalar.dma_start(T.hraw[16:32, :], T.hh[:, :]).then_inc(T.sem.hl, 16)
    h = COLS // 2
    g.sync.dma_start(T.xs[:, 0:h], T.x[:, 0:h]).then_inc(T.sem.xl, 16)
    g.scalar.dma_start(T.xs[:, h:COLS], T.x[:, h:COLS]).then_inc(T.sem.xl, 16)
    n, inc, sync = _counted(T, v)
    g.iota(T.pi[:, 0:1], [[0, 1]], 0, 1).then_inc(T.sem.gk, 1)
    g.iota(T.mm[:, :], [[1, LC]], 0, 0).then_inc(T.sem.ga, 1)
    v.wait_ge(T.sem.gk, 1)
    inc(v.tensor_scalar(T.pm[:, 0:1], T.pi[:, 0:1], 15, None, op.bitwise_and))
    sync()
    g.wait_ge(T.sem.vs, 1)
    to = [c for c in hp if c in P["hnext"]]
    eng = dict((c, _hh_engines(P, core, c, _bits(topo.mask(core, c)))) for c in to)
    g.remote_dma_fused([_xfer(T, topo, core, c, _or(eng[c]), T.sem.hm, T.pm[:, 0:1], T.hp[:, 2:3]) for c in to],
                       local_sem=T.sem.ls)
    inc(v.tensor_copy(T.pk[:, 0:1], T.pi[:, 0:1]))
    v.memset(T.hraw[32:64, :], 0).then_inc(T.sem.vz, 1)
    v.memset(T.hraw[64:128, :], 0).then_inc(T.sem.vz, 1)
    v.wait_ge(T.sem.ga, 1)
    inc(v.tensor_scalar(T.m4[:, :], T.mm[:, :], 4, None, op.arith_shift_right))
    inc(v.tensor_copy(T.pf[:, 0:1], T.pm[:, 0:1]))
    sync()
    inc(v.tensor_scalar(T.oh[:, :], T.m4[:, :], T.pk[:, 0:1], None, op.is_equal))
    inc(v.tensor_scalar(T.jp[:, :], T.mm[:, :], 16.0, T.pf[:, 0:1], op.mult, op.add))
    sync()
    g.wait_ge(T.sem.vz, 2)
    g.wait_ge(T.sem.hl, 32)
    g.remote_dma_fused([_xfer(T, topo, core, c, _or(eng[c]), T.sem.hs, T.hraw[:, :], T.hp[:, 0:2]) for c in to],
                       local_sem=T.sem.ls)
    ls = 2 * sum(len(eng[c]) for c in to)
    v.wait_ge(T.sem.hl, 32)
    inc(v.tensor_copy(T.rhs[0:16, 0:1], T.hraw[0:16, 0:1]))
    g.tensor.wait_ge(T.sem.vs, n[0])
    g.tensor.matmul(T.ps[:, 0:1], T.oh[0:16, :], T.rhs[0:16, 0:1], True, True).then_inc(T.sem.ms, 1)
    v.wait_ge(T.sem.ms, 1)
    inc(v.tensor_scalar(T.ic[:, :], T.jp[:, :], T.ps[:, 0:1], None, op.add))
    sync()
    inc(v.tensor_scalar(T.id2[:, :], T.ic[:, :], COLS - 1, None, op.bitwise_and))
    sync()
    inc(v.tensor_copy(T.off[:, :], T.id2[:, :]))
    units = [P["unit_of"][c][1] for c in hp + [core]]
    a, b = P["calls"][core][0][0]
    parts = [(u * UW, u * UW + UW // 2, UW // 2) for u in units]
    lo = P["calls"][hp[2]][0][0][0] * W
    parts[2:3] = [(lo, lo + PART * W // 2, PART * W // 2), (a * W, b * W, W)]
    for k, (queue, isv) in enumerate(((v, True), (g.scalar, False))):
        queue.wait_ge(T.sem.vs, n[0])
        queue.wait_ge(T.sem.xl, 32)
        for i, pt in enumerate(parts):
            lo = pt[k]
            hi = lo + pt[2]
            _turn(queue, isv, T.w[:, lo:hi], T.xs[:, :], T.off[:, lo // 16:hi // 16],
                  T.sem[("gv%d" if isv else "gs%d") % i])

    def turned(i):
        g.wait_ge(T.sem["gv%d" % i], 1)
        g.wait_ge(T.sem["gs%d" % i], 1)

    for i in range(3):
        turned(i)
        lo, wd = parts[i][0], 2 * parts[i][2]
        e = _unit_engines(topo, P, core, i)
        rid, pid = topo.addr(hp[i], core)
        g.remote_dma(T.rx[:, 0:wd], T.w[:, lo:lo + wd], T.sem.xr, T.sem.ls, pid, rid, _or(e))
        ls += len(e)
    for k, (slices, ne) in enumerate(P["calls"][core]):
        turned(3 + k)
        ls += _send_slices(g, core, T, topo, P, ri, slices, ne, T.w, 0)
    for q, sem, ks in ((g.sync, T.sem.st, (1, 0, 2)), (g.scalar, T.sem.su, (3, 4))):
        stores = 0
        for k in ks:
            first, cnt, ne = _steps()[k]
            blocks = sorted((ri // 2 - first - i) % NP for i in range(cnt))
            need = sum(ne * (BOUNDS[b + 1] - BOUNDS[b]) for b in blocks)
            if k == 0:
                need = len(_bits(topo.mask(P["gate"][core], core)))
            q.wait_ge(T.sem["za%d" % k], need)
            runs = [[blocks[0], blocks[0] + 1]]
            for b in blocks[1:]:
                if b == runs[-1][1]:
                    runs[-1][1] = b + 1
                else:
                    runs.append([b, b + 1])
            for b0, b1 in runs:
                lo, hi = BOUNDS[b0] * W, BOUNDS[b1] * W
                q.dma_start(T.y[:, lo:hi], T.z[:, lo:hi]).then_inc(sem, 16)
                stores += 1
        q.wait_ge(sem, 16 * stores)
    g.wait_ge(T.sem.ls, ls)


def _helper(g, core, T, topo, P):
    ri = P["unit_of"][core][0]
    r = P["ranks"][ri]
    i = P["helpers"][r].index(core)
    d = [c for c in P["cols"] if core in P["cols"][c]][0]
    ls = _columns(g, core, T, topo, P, d)
    if core in P["hnext"]:
        e = len(_hh_engines(P, r, core, _bits(topo.mask(r, core))))
        g.wait_ge(T.sem.hm, e)
        g.wait_ge(T.sem.hs, e)
        rid, pid = topo.addr(d, core)
        m = topo.mask(core, d)
        g.remote_dma(T.hp[:, :], T.hp[:, :], T.sem.hs, T.sem.ls, pid, rid, m)
        ls += len(_bits(m))
    g.wait_ge(T.sem.xr, len(_unit_engines(topo, P, r, i)))
    first = P["calls"][core][0][0][0]
    for slices, ne in P["calls"][core]:
        ls += _send_slices(g, core, T, topo, P, ri, slices, ne, T.rx, first)
    g.wait_ge(T.sem.ls, ls)


def _rotator(g, core, T, topo, P):
    j = P["rot"].index(core)
    nv, ls = _rotator_list(g, core, T, topo, P, j)
    da = 0
    for c in P["calls"]:
        for slices, ne in P["calls"][c]:
            if j in slices:
                da += ne
    o0 = 2 * sum(STEPS)
    parts = [(2 * first, 2 * cnt) for first, cnt, _ne in _steps()[:len(STEPS)]]
    parts.insert(1, (o0, NR - o0))
    for k, (queue, isv) in enumerate(((g.vector, True), (g.scalar, False))):
        queue.wait_ge(T.sem.vs, nv)
        queue.wait_ge(T.sem.da, da)
        for i, (o, cnt) in enumerate(parts):
            a = o + k * cnt // 2
            b = a + cnt // 2
            _turn(queue, isv, T.wout[:, a * W:b * W], T.win[:, :], T.off[:, a * W // 16:b * W // 16],
                  T.sem[("gv%d" if isv else "gs%d") % i])
    for i in range(len(parts)):
        g.wait_ge(T.sem["gv%d" % i], 1)
        g.wait_ge(T.sem["gs%d" % i], 1)
        if i == 1:
            d = P["second"][core]
            e = _relay_engines(topo, P, core)
            rid, pid = topo.addr(d, core)
            g.remote_dma(T.rx[:, 0:(NR - o0) * W], T.wout[:, o0 * W:NR * W], T.sem.xr, T.sem.ls, pid, rid, _or(e))
            ls += len(e)
        else:
            ls += _send_step(g, core, T, topo, P, j, i - (i > 1), T.wout, 0)
    g.wait_ge(T.sem.ls, ls)


def _second(g, core, T, topo, P):
    r = [c for c in P["rot"] if P["second"][c] == core][0]
    ls = _columns(g, core, T, topo, P, r)
    g.wait_ge(T.sem.xr, len(_relay_engines(topo, P, r)))
    for k in range(len(MORE)):
        ls += _send_step(g, core, T, topo, P, P["rot"].index(r), len(STEPS) + k, T.rx, 2 * sum(STEPS))
    for ri, d in enumerate(P["ranks"]):
        if P["gate"][d] == core:
            b = ri // 2
            g.wait_ge(T.sem.za0, _steps()[0][2] * (BOUNDS[b + 1] - BOUNDS[b]))
            lo, hi = BOUNDS[b] * W, BOUNDS[b + 1] * W
            rid, pid = topo.addr(d, core)
            m = topo.mask(core, d)
            g.remote_dma(T.z[:, lo:hi], T.z[:, lo:hi], T.sem.za0, T.sem.ls, pid, rid, m)
            ls += len(_bits(m))
    g.wait_ge(T.sem.ls, ls)


def rank_program(g, core, T, topo):
    P = _plan(T, topo)
    if core in P["ranks"]:
        _rank(g, core, T, topo, P)
    elif core in P["unit_of"]:
        _helper(g, core, T, topo, P)
    elif core in P["rot"]:
        _rotator(g, core, T, topo, P)
    elif core in P["second"].values():
        _second(g, core, T, topo, P)
